import numpy as np
import ml_dtypes


def mxq(x, axis, fmt="e4m3"):
    dtype, down = {"e4m3": (ml_dtypes.float8_e4m3fn, 7), "e5m2": (ml_dtypes.float8_e5m2, 14)}[fmt]
    v = np.moveaxis(np.asarray(x, np.float32).astype(ml_dtypes.bfloat16).astype(np.float64), axis, -1)
    blocks = v.reshape(v.shape[:-1] + (-1, 32))
    amax = np.abs(blocks).max(-1, keepdims=True)
    byte = np.maximum(np.where(amax > 0, np.frexp(amax)[1] - 1 + 127, 0) - down, 1)
    scale = np.exp2(byte - 127.0)
    codes = (blocks / scale).astype(np.float32).astype(dtype).astype(np.float64)
    return np.moveaxis((codes * scale).reshape(v.shape), -1, axis)


WIDE = False


def mx_kscale(k):
    if not WIDE:
        return np.ones(k)
    levels = np.array([24, -24, 12, -12, 0])
    if k % 512:
        return np.exp2(np.random.permutation(np.resize(levels, k // 32))).repeat(32)
    a = np.empty((k // 512, 16))
    for p in range(k // 512):
        a[p, :8] = np.random.permutation(np.resize(levels, 8))
        for g in range(8):
            far = levels[np.abs(levels - a[p, g]) >= 10]
            a[p, g + 8] = far[np.random.randint(len(far))]
    return np.exp2(a.ravel()).repeat(32)


def f64(x):
    return np.asarray(x).astype(np.float64)


def striped(idx):
    return np.tile(idx.reshape(-1, 16).T, (8, 1)).astype(np.uint16)


def unstriped(offs):
    return offs[:16].T.reshape(-1).astype(np.int64)


E2M1 = np.array([0.0, 0.5, 1.0, 1.5, 2.0, 3.0, 4.0, 6.0, -0.0, -0.5, -1.0, -1.5, -2.0, -3.0, -4.0, -6.0])


def pack_weight(w, fmt):
    k, n = w.shape
    w = f64(np.asarray(w, np.float32).astype(ml_dtypes.bfloat16)).reshape(k // 32, 32, n)
    amax = np.abs(w).max(1)
    if fmt == "e4m3":
        byte = np.frexp(amax)[1] - 1 + 127 - 7
    else:
        mant, ex = np.frexp(amax / 6.0)
        byte = np.where(mant > 0.5, ex, ex - 1) + 127
    byte = np.clip(np.where(amax > 0, byte, 1), 1, 254)
    scaled = (w * np.exp2(127.0 - byte)[:, None, :]).reshape(k, n).astype(np.float32)
    by_word = np.ascontiguousarray(scaled.reshape(k // 512, 128, 4, n).transpose(0, 1, 3, 2))
    if fmt == "e4m3":
        words = by_word.astype(ml_dtypes.float8_e4m3fn).view(np.uint8)
    else:
        c = by_word.astype(ml_dtypes.float4_e2m1fn).view(np.uint8) & 0xF
        words = (c[..., 0::2] | (c[..., 1::2] << 4)).reshape(k // 512, 128, 2 * n)
    return np.ascontiguousarray(words), np.ascontiguousarray(byte.astype(np.uint8).reshape(k // 512, 16, n))


def unpack_weight(words, scales, fmt):
    g, _, n = scales.shape
    words = np.ascontiguousarray(words).reshape(g, 128, n, -1)
    if fmt == "e4m3":
        vals = words.view(ml_dtypes.float8_e4m3fn).astype(np.float64)
    else:
        nib = np.empty((g, 128, n, 4), np.uint8)
        nib[..., 0::2] = words & 0xF
        nib[..., 1::2] = words >> 4
        vals = E2M1[nib]
    vals = vals * np.repeat(np.exp2(scales.astype(np.float64) - 127.0), 8, axis=1)[..., None]
    return vals.transpose(0, 1, 3, 2).reshape(g * 512, n)


def pack_table4(v):
    words, scales = pack_weight(v, "e2m1")
    g, t = words.shape[0] // 2, v.shape[1]
    return np.ascontiguousarray(words.reshape(g, 2, 128, t, 2).transpose(0, 2, 3, 1, 4).reshape(g, 128, t, 4)), scales


def unpack_table4(words, scales):
    g, _, t, _ = words.shape
    return unpack_weight(words.reshape(g, 128, t, 2, 2).transpose(0, 3, 1, 2, 4).reshape(2 * g, 128, 2 * t), scales, "e2m1")


def planes(y):
    n, m = y.shape
    v = y.astype(np.float32).astype(ml_dtypes.bfloat16).astype(np.float64).reshape(n // 32, 32, m)
    top = np.abs(v).max(1)
    byte = np.clip(np.where(top > 0, np.frexp(top)[1] - 1 + 127 - 7, 1), 1, 254)
    codes = (v * np.exp2(127.0 - byte)[:, None, :]).reshape(n, m).astype(np.float32).astype(ml_dtypes.float8_e4m3fn).view(np.uint8)
    words = codes.reshape(n // 512, 128, 4, m).transpose(0, 1, 3, 2)
    return np.ascontiguousarray(words), np.ascontiguousarray(byte.astype(np.uint8).reshape(n // 512, 16, m))


def gelu(f):
    return 0.5 * f * (1.0 + np.tanh(np.sqrt(2.0 / np.pi) * (f + 0.044715 * f**3)))


K, R, N, T, J = 1024, 512, 512, 2048, 1024


def setup_inputs():
    n = np.random.standard_normal
    s = mx_kscale(K)[:, None]
    u = mx_kscale(R)[:, None]
    p_tab = pack_table4(n((K, T)) * s)
    p_wg = pack_weight(n((K, R)) / np.sqrt(K) / s, "e2m1")
    return {
        "tab_words": p_tab[0],
        "tab_scales": p_tab[1],
        "wg_words": p_wg[0],
        "wg_scales": p_wg[1],
        "wu": (n((K, R)) / np.sqrt(K) / s * u.T).astype(np.float32),
        "wd": (n((R, N)) / np.sqrt(R) / u).astype(np.float32),
        "wgo": np.tile(np.random.uniform(0.5, 2.0, J), (128, 1)).astype(np.float32),
        "offs": striped(np.random.permutation(T)[:J]),
    }


def reference(tab_words, tab_scales, wg_words, wg_scales, wu, wd, wgo, offs):
    idx = unstriped(offs)
    tab_ = unpack_table4(tab_words, tab_scales)[:, idx]
    wg_ = unpack_weight(wg_words, wg_scales, "e2m1")
    wu_ = mxq(f64(wu), 0, "e4m3")
    ga = wg_.T @ tab_
    ub = wu_.T @ tab_
    h = gelu(ga) * ub
    h_ = mxq(h, 0, "e4m3")
    wd_ = mxq(f64(wd), 0, "e4m3")
    y = wd_.T @ h_
    out = np.zeros((N, T))
    out[:, idx] = f64(wgo)[0] * (y)
    return (out,) + planes(out)

@@ -1,0 +1,215 @@
+from contextlib import ExitStack
+
+import concourse.mybir as mybir
+
+K, R, N, T, J = 1024, 512, 512, 2048, 1024
+FLOPS = 2 * J * (2 * K * R + R * N)
+
+F32 = mybir.dt.float32
+BF16 = mybir.dt.bfloat16
+I32 = mybir.dt.int32
+U32 = mybir.dt.uint32
+U16 = mybir.dt.uint16
+U8 = mybir.dt.uint8
+FP8X4 = mybir.dt.float8_e4m3fn_x4
+FP4X4 = mybir.dt.float4_e2m1fn_x4
+MULT = mybir.AluOpType.mult
+GELU = mybir.ActivationFunctionType.Gelu_apprx_tanh
+
+P = 128
+PACK = 4
+PASSES = K // (P * PACK)
+CHUNK = 256
+SUB = 128
+OUT_CHUNK = 512
+
+
+def tile_list_modp_ggelu_noneP_kernel(
+    tc, tab_words, tab_scales, wg_words, wg_scales, wu, wd, wgo, offs, out_0, out_1, out_2
+):
+    nc = tc.nc
+    with ExitStack() as ctx:
+        keep = ctx.enter_context(tc.tile_pool(name="keep", bufs=1))
+        ring = ctx.enter_context(tc.tile_pool(name="ring", bufs=2))
+        psum = ctx.enter_context(tc.psum_pool(name="psum", bufs=1))
+
+        def held(shape, dtype, name, tag=None):
+            return keep.tile(shape, dtype, name=name, tag=tag or name, align_bytes=64)
+
+        offsets = keep.tile([P, J // 16], U16, name="offsets")
+        nc.sync.dma_start(offsets[:], offs)
+
+        tab_w = held([P, T], U32, "tab_w")
+        nc.sync.dma_start(tab_w[:].bitcast(I32), tab_words[0].rearrange("p t b -> p (t b)").bitcast(I32))
+
+        tab_s = held([P, PASSES, T], U8, "tab_s")
+        nc.vector.memset(tab_s[:].rearrange("p a t -> p (a t)").bitcast(I32), 0)
+        for q in range(4):
+            nc.scalar.dma_start(
+                tab_s[32 * q : 32 * q + 4, :, :].bitcast(I32),
+                tab_scales[:, 4 * q : 4 * q + 4, :].rearrange("a r t -> r a t").bitcast(I32),
+            )
+        warm = held([P, 8], F32, "warm", "wu1_raw")
+        warm2 = held([P, 8], F32, "warm2", "wd_raw")
+        nc.vector.memset(warm[:], 0.0)
+        nc.scalar.activation(warm2[:], warm[:], GELU)
+
+        wg_raw = held([P, PASSES, 2 * R], U8, "wg_raw")
+        nc.sync.dma_start(wg_raw[:].bitcast(I32), wg_words.rearrange("a p c -> p a c").bitcast(I32))
+        wgs_raw = held([P, PASSES, R], U8, "wgs_raw")
+        nc.gpsimd.memset(wgs_raw[:].rearrange("p a c -> p (a c)").bitcast(I32), 0)
+        for q in range(4):
+            nc.gpsimd.dma_start(
+                wgs_raw[32 * q : 32 * q + 4, :, :].bitcast(I32),
+                wg_scales[:, 4 * q : 4 * q + 4, :].rearrange("a r c -> r a c").bitcast(I32),
+            )
+
+        raws = []
+        for name, src in (("wu0", wu[0:512, :]), ("wu1", wu[512:1024, :]), ("wd", wd)):
+            raw = held([P, PACK, 512], F32, name + "_raw")
+            nc.sync.dma_start(raw[:], src.rearrange("(p j) c -> p j c", j=PACK))
+            raws.append(raw)
+        windows = [held([P, T], F32, "window%d" % t) for t in range(2)]
+        for t in range(2):
+            nc.vector.memset(windows[t][:], 0.0)
+
+        tok_w, tok_s = [], []
+        for c in range(J // CHUNK):
+            offs_c = offsets[:, c * CHUNK // 16 : (c + 1) * CHUNK // 16]
+            both = held([P, CHUNK], U32, "both%d" % c)
+            nc.vector.tensor_copy(both[:], tab_w[:].indirect(offs_c))
+            scal = [held([P, CHUNK], U8, "tok_s%d_%d" % (c, a)) for a in range(PASSES)]
+            for a in range(PASSES):
+                nc.vector.tensor_copy(scal[a][:], tab_s[:, a, :].indirect(offs_c))
+            parted = held([P, PASSES, 2 * CHUNK], U8, "tok_w%d" % c)
+            nc.vector.tensor_copy(
+                parted[:].bitcast(U16), both[:].bitcast(U16).rearrange("p (j a) -> p a j", a=PASSES)
+            )
+            tok_w.append(parted)
+            tok_s.append(scal)
+            if c == 0:
+                wg_w = held([P, PASSES, 2 * R], U8, "wg_w")
+                nc.vector.tensor_copy(
+                    wg_w[:].bitcast(U16).rearrange("p a (t m) -> p a t m", t=PACK),
+                    wg_raw[:].bitcast(U16).rearrange("p a (m t) -> p a t m", t=PACK),
+                )
+                wg_s = held([P, PASSES, R], U8, "wg_s")
+                nc.vector.tensor_copy(
+                    wg_s[:].rearrange("p a (t m) -> p a t m", t=PACK),
+                    wgs_raw[:].rearrange("p a (m t) -> p a t m", t=PACK),
+                )
+
+        gate = held([P, J], F32, "gate", "wgs_raw")
+        nc.sync.dma_start(gate[:], wgo)
+        codes, scales = [], []
+        for i, raw in enumerate(raws):
+            grouped = held([P, PACK * 512], BF16, "grouped%d" % i)
+            nc.scalar.copy(
+                grouped[:].rearrange("p (t m j) -> p m j t", t=PACK, j=PACK),
+                raw[:].rearrange("p j (m t) -> p m j t", t=PACK),
+            )
+            cod = held([P, 512], U32, "codes%d" % i)
+            sca = held([P, 512], U8, "scales%d" % i)
+            nc.vector.quantize_mx(out=cod[:].bitcast(FP8X4), scales=sca[:], in_=grouped[:])
+            codes.append(cod)
+            scales.append(sca)
+
+        for t in range(2, PACK):
+            win = held([P, T], F32, "window%d" % t, ("wd_raw", "grouped2")[t - 2])
+            nc.gpsimd.memset(win[:], 0.0)
+            windows.append(win)
+        y_late = held([P, 2, J], F32, "y_late")
+        for c in range(J // CHUNK):
+            h_b = ring.tile([P, CHUNK * PACK], BF16, name="h_b", align_bytes=64)
+            for s in range(CHUNK // SUB):
+                cols = slice(s * SUB, (s + 1) * SUB)
+                wcols = slice(2 * s * SUB, 2 * (s + 1) * SUB)
+                ga = psum.tile([P, PACK, SUB], F32, name="ga", bufs=2)
+                ub = psum.tile([P, PACK, SUB], F32, name="ub", bufs=3)
+                for t in range(PACK):
+                    for a in range(PASSES):
+                        nc.tensor.matmul_mx(
+                            out=ga[:, t, :],
+                            lhsT=wg_w[:, a, 2 * P * t : 2 * P * (t + 1)].bitcast(FP4X4),
+                            lhsT_scale=wg_s[:, a, P * t : P * (t + 1)],
+                            rhs=tok_w[c][:, a, wcols].bitcast(FP4X4),
+                            rhs_scale=tok_s[c][a][:, cols],
+                            start=(a == 0),
+                            stop=(a == PASSES - 1),
+                        )
+                act = ring.tile([P, SUB, PACK], F32, name="act", bufs=3)
+                nc.scalar.activation(act[:], ga[:].rearrange("p t j -> p j t"), GELU)
+                for t in range(PACK):
+                    for a in range(PASSES):
+                        nc.tensor.matmul_mx(
+                            out=ub[:, t, :],
+                            lhsT=codes[a][:, P * t : P * (t + 1)].bitcast(FP8X4),
+                            lhsT_scale=scales[a][:, P * t : P * (t + 1)],
+                            rhs=tok_w[c][:, a, wcols].bitcast(FP4X4),
+                            rhs_scale=tok_s[c][a][:, cols],
+                            start=(a == 0),
+                            stop=(a == PASSES - 1),
+                        )
+                nc.vector.tensor_tensor(
+                    h_b[:, s * SUB * PACK : (s + 1) * SUB * PACK].rearrange("p (j t) -> p j t", t=PACK),
+                    ub[:].rearrange("p t j -> p j t"),
+                    act[:],
+                    MULT,
+                )
+            h_c = ring.tile([P, CHUNK], U32, name="h_c", align_bytes=64)
+            h_s = ring.tile([P, CHUNK], U8, name="h_s", align_bytes=64)
+            nc.vector.quantize_mx(out=h_c[:].bitcast(FP8X4), scales=h_s[:], in_=h_b[:])
+            tok = slice(c * CHUNK, (c + 1) * CHUNK)
+            for u in range(2):
+                yb = psum.tile([P, 2, CHUNK], F32, name="yb", bufs=3)
+                for e in range(2):
+                    t = 2 * u + e
+                    nc.tensor.matmul_mx(
+                        out=yb[:, e, :],
+                        lhsT=codes[2][:, P * t : P * (t + 1)].bitcast(FP8X4),
+                        lhsT_scale=scales[2][:, P * t : P * (t + 1)],
+                        rhs=h_c[:].bitcast(FP8X4),
+                        rhs_scale=h_s[:],
+                        start=True,
+                        stop=True,
+                    )
+                if u == 0:
+                    y_early = ring.tile([P, 2, CHUNK], F32, name="y_early")
+                    nc.scalar.copy(y_early[:], yb[:])
+                    for e in range(2):
+                        nc.vector.tensor_tensor(
+                            windows[e][:].indirect(offsets[:, c * CHUNK // 16 : (c + 1) * CHUNK // 16]),
+                            y_early[:, e, :],
+                            gate[:, tok],
+                            MULT,
+                        )
+                else:
+                    nc.scalar.copy(y_late[:, :, tok], yb[:])
+
+        rows = out_0.rearrange("(p t) c -> t p c", t=PACK)
+        n_out = T // OUT_CHUNK
+        pairs = [held([P, 2, OUT_CHUNK, 2], BF16, "pairs%d" % o) for o in range(n_out)]
+        for t in range(PACK):
+            if t >= 2:
+                nc.vector.tensor_tensor(windows[t][:].indirect(offsets[:]), y_late[:, t - 2, :], gate[:], MULT)
+            nc.sync.dma_start(rows[t], windows[t][:])
+            for o in range(n_out):
+                nc.scalar.copy(pairs[o][:, t // 2, :, t % 2], windows[t][:, o * OUT_CHUNK : (o + 1) * OUT_CHUNK])
+
+        out_s = held([P, T], U8, "out_s")
+        for o in range(n_out):
+            ocols = slice(o * OUT_CHUNK, (o + 1) * OUT_CHUNK)
+            fin = held([P, OUT_CHUNK * PACK], BF16, "fin%d" % o)
+            nc.vector.tensor_copy(
+                fin[:].bitcast(I32).rearrange("p (c u) -> p c u", u=2),
+                pairs[o][:].rearrange("p u c e -> p u (c e)").bitcast(I32).rearrange("p u c -> p c u"),
+            )
+            out_c = held([P, OUT_CHUNK], U32, "out_c%d" % o)
+            nc.vector.quantize_mx(out=out_c[:].bitcast(FP8X4), scales=out_s[:, ocols], in_=fin[:])
+            nc.sync.dma_start(
+                out_1[0].rearrange("p t b -> p (t b)").bitcast(I32)[:, ocols], out_c[:].bitcast(I32)
+            )
+        for q in range(4):
+            (nc.sync if q % 2 else nc.scalar).dma_start(
+                out_2[0, 4 * q : 4 * q + 4, :].bitcast(I32), out_s[32 * q : 32 * q + 4, :].bitcast(I32)
+            )

@@ -21,7 +21,7 @@ PACK = 4
 PASSES = K // (P * PACK)
 CHUNK = 256
 SUB = 128
-OUT_CHUNK = 512
+OUT_WIDTHS = (256, 512, 512, 512, 256)
 
 
 def tile_list_modp_ggelu_noneP_kernel(
@@ -39,54 +39,57 @@ def tile_list_modp_ggelu_noneP_kernel(
         offsets = keep.tile([P, J // 16], U16, name="offsets")
         nc.sync.dma_start(offsets[:], offs)
 
+        tab_s = held([P, T], U8, "tab_s")
+        nc.sync.dma_start(tab_s[0:32, :].bitcast(I32), tab_scales.rearrange("a q t -> (a q) t").bitcast(I32))
         tab_w = held([P, T], U32, "tab_w")
         nc.sync.dma_start(tab_w[:].bitcast(I32), tab_words[0].rearrange("p t b -> p (t b)").bitcast(I32))
-
-        tab_s = held([P, PASSES, T], U8, "tab_s")
-        nc.vector.memset(tab_s[:].rearrange("p a t -> p (a t)").bitcast(I32), 0)
-        for q in range(4):
-            nc.scalar.dma_start(
-                tab_s[32 * q : 32 * q + 4, :, :].bitcast(I32),
-                tab_scales[:, 4 * q : 4 * q + 4, :].rearrange("a r t -> r a t").bitcast(I32),
-            )
-        warm = held([P, 8], F32, "warm", "wu1_raw")
-        warm2 = held([P, 8], F32, "warm2", "wd_raw")
-        nc.vector.memset(warm[:], 0.0)
-        nc.scalar.activation(warm2[:], warm[:], GELU)
-
         wg_raw = held([P, PASSES, 2 * R], U8, "wg_raw")
         nc.sync.dma_start(wg_raw[:].bitcast(I32), wg_words.rearrange("a p c -> p a c").bitcast(I32))
+
+        def load_rows(src, name, tag=None):
+            raw = held([P, PACK, 512], F32, name, tag)
+            nc.sync.dma_start(raw[:], src.rearrange("(p j) c -> p j c", j=PACK))
+            return raw
+
+        wu0_raw = load_rows(wu[0:512, :], "wu0_raw")
+
         wgs_raw = held([P, PASSES, R], U8, "wgs_raw")
-        nc.gpsimd.memset(wgs_raw[:].rearrange("p a c -> p (a c)").bitcast(I32), 0)
+        nc.vector.memset(wgs_raw[:].rearrange("p a c -> p (a c)").bitcast(I32), 0)
         for q in range(4):
-            nc.gpsimd.dma_start(
+            nc.scalar.dma_start(
                 wgs_raw[32 * q : 32 * q + 4, :, :].bitcast(I32),
                 wg_scales[:, 4 * q : 4 * q + 4, :].rearrange("a r c -> r a c").bitcast(I32),
             )
+        nc.vector.memset(tab_s[32:64, :].bitcast(I32), 0)
+        nc.vector.memset(tab_s[64:128, :].bitcast(I32), 0)
+        warm = held([P, 8], F32, "warm")
+        warm2 = held([P, 8], F32, "warm2")
+        nc.vector.memset(warm[:], 0.0)
+        nc.scalar.activation(warm2[:], warm[:], GELU)
+        tok_s = held([P, PASSES, J], U8, "tok_s")
+        nc.vector.memset(tok_s[:].rearrange("p a j -> p (a j)").bitcast(I32), 0)
 
-        raws = []
-        for name, src in (("wu0", wu[0:512, :]), ("wu1", wu[512:1024, :]), ("wd", wd)):
-            raw = held([P, PACK, 512], F32, name + "_raw")
-            nc.sync.dma_start(raw[:], src.rearrange("(p j) c -> p j c", j=PACK))
-            raws.append(raw)
-        windows = [held([P, T], F32, "window%d" % t) for t in range(2)]
-        for t in range(2):
-            nc.vector.memset(windows[t][:], 0.0)
+        picked_s = held([P, J], U8, "picked_s")
+        nc.vector.tensor_copy(picked_s[:], tab_s[:].indirect(offsets[:]))
+        wu1_raw = load_rows(wu[512:1024, :], "wu1_raw", "tab_s")
+        for a in range(PASSES):
+            for q in range(4):
+                (nc.gpsimd if q == 3 else nc.sync).dma_start(
+                    tok_s[32 * q : 32 * q + 4, a, :].bitcast(I32),
+                    picked_s[16 * a + 4 * q : 16 * a + 4 * q + 4, :].bitcast(I32),
+                )
+        windows = [held([P, T], F32, "window0", "warm")]
+        nc.gpsimd.memset(windows[0][:], 0.0)
 
-        tok_w, tok_s = [], []
+        tok_w = []
         for c in range(J // CHUNK):
-            offs_c = offsets[:, c * CHUNK // 16 : (c + 1) * CHUNK // 16]
             both = held([P, CHUNK], U32, "both%d" % c)
-            nc.vector.tensor_copy(both[:], tab_w[:].indirect(offs_c))
-            scal = [held([P, CHUNK], U8, "tok_s%d_%d" % (c, a)) for a in range(PASSES)]
-            for a in range(PASSES):
-                nc.vector.tensor_copy(scal[a][:], tab_s[:, a, :].indirect(offs_c))
+            nc.vector.tensor_copy(both[:], tab_w[:].indirect(offsets[:, c * CHUNK // 16 : (c + 1) * CHUNK // 16]))
             parted = held([P, PASSES, 2 * CHUNK], U8, "tok_w%d" % c)
             nc.vector.tensor_copy(
                 parted[:].bitcast(U16), both[:].bitcast(U16).rearrange("p (j a) -> p a j", a=PASSES)
             )
             tok_w.append(parted)
-            tok_s.append(scal)
             if c == 0:
                 wg_w = held([P, PASSES, 2 * R], U8, "wg_w")
                 nc.vector.tensor_copy(
@@ -98,31 +101,37 @@ def tile_list_modp_ggelu_noneP_kernel(
                     wg_s[:].rearrange("p a (t m) -> p a t m", t=PACK),
                     wgs_raw[:].rearrange("p a (m t) -> p a t m", t=PACK),
                 )
-
-        gate = held([P, J], F32, "gate", "wgs_raw")
+        wd_raw = load_rows(wd, "wd_raw", "both0")
+        gate = held([P, J], F32, "gate", "both1")
         nc.sync.dma_start(gate[:], wgo)
-        codes, scales = [], []
-        for i, raw in enumerate(raws):
-            grouped = held([P, PACK * 512], BF16, "grouped%d" % i)
-            nc.scalar.copy(
-                grouped[:].rearrange("p (t m j) -> p m j t", t=PACK, j=PACK),
-                raw[:].rearrange("p j (m t) -> p m j t", t=PACK),
-            )
-            cod = held([P, 512], U32, "codes%d" % i)
-            sca = held([P, 512], U8, "scales%d" % i)
-            nc.vector.quantize_mx(out=cod[:].bitcast(FP8X4), scales=sca[:], in_=grouped[:])
-            codes.append(cod)
-            scales.append(sca)
 
-        for t in range(2, PACK):
-            win = held([P, T], F32, "window%d" % t, ("wd_raw", "grouped2")[t - 2])
-            nc.gpsimd.memset(win[:], 0.0)
-            windows.append(win)
-        y_late = held([P, 2, J], F32, "y_late")
-        for c in range(J // CHUNK):
+        def quantise_half(raw, u, copy, name):
+            grouped = held([P, 2 * P * PACK], BF16, name + "_grouped")
+            copy(
+                grouped[:].rearrange("p (t m j) -> p m j t", t=2, j=PACK),
+                raw[:].rearrange("p j (m t) -> p m j t", t=PACK)[:, :, :, 2 * u : 2 * u + 2],
+            )
+            cod = held([P, 2 * P], U32, name + "_codes")
+            sca = held([P, 2 * P], U8, name + "_scales")
+            nc.vector.quantize_mx(out=cod[:].bitcast(FP8X4), scales=sca[:], in_=grouped[:])
+            return cod, sca
+
+        wu_q = [
+            [quantise_half(wu0_raw, 0, nc.scalar.copy, "wu00"), quantise_half(wu0_raw, 1, nc.scalar.copy, "wu01")],
+            [quantise_half(wu1_raw, 0, nc.scalar.copy, "wu10"), quantise_half(wu1_raw, 1, nc.vector.tensor_copy, "wu11")],
+        ]
+        windows.append(held([P, T], F32, "window1", "wu11_grouped"))
+        nc.vector.memset(windows[1][:], 0.0)
+
+        def stationary(halves, t):
+            cod, sca = halves[t // 2]
+            cols = slice(P * (t % 2), P * (t % 2 + 1))
+            return cod[:, cols].bitcast(FP8X4), sca[:, cols]
+
+        def hidden(c):
             h_b = ring.tile([P, CHUNK * PACK], BF16, name="h_b", align_bytes=64)
             for s in range(CHUNK // SUB):
-                cols = slice(s * SUB, (s + 1) * SUB)
+                scale_cols = slice(c * CHUNK + s * SUB, c * CHUNK + (s + 1) * SUB)
                 wcols = slice(2 * s * SUB, 2 * (s + 1) * SUB)
                 ga = psum.tile([P, PACK, SUB], F32, name="ga", bufs=2)
                 ub = psum.tile([P, PACK, SUB], F32, name="ub", bufs=3)
@@ -133,20 +142,21 @@ def tile_list_modp_ggelu_noneP_kernel(
                             lhsT=wg_w[:, a, 2 * P * t : 2 * P * (t + 1)].bitcast(FP4X4),
                             lhsT_scale=wg_s[:, a, P * t : P * (t + 1)],
                             rhs=tok_w[c][:, a, wcols].bitcast(FP4X4),
-                            rhs_scale=tok_s[c][a][:, cols],
+                            rhs_scale=tok_s[:, a, scale_cols],
                             start=(a == 0),
                             stop=(a == PASSES - 1),
                         )
-                act = ring.tile([P, SUB, PACK], F32, name="act", bufs=3)
+                act = ring.tile([P, SUB, PACK], F32, name="act")
                 nc.scalar.activation(act[:], ga[:].rearrange("p t j -> p j t"), GELU)
                 for t in range(PACK):
                     for a in range(PASSES):
+                        w_codes, w_scales = stationary(wu_q[a], t)
                         nc.tensor.matmul_mx(
                             out=ub[:, t, :],
-                            lhsT=codes[a][:, P * t : P * (t + 1)].bitcast(FP8X4),
-                            lhsT_scale=scales[a][:, P * t : P * (t + 1)],
+                            lhsT=w_codes,
+                            lhsT_scale=w_scales,
                             rhs=tok_w[c][:, a, wcols].bitcast(FP4X4),
-                            rhs_scale=tok_s[c][a][:, cols],
+                            rhs_scale=tok_s[:, a, scale_cols],
                             start=(a == 0),
                             stop=(a == PASSES - 1),
                         )
@@ -156,58 +166,78 @@ def tile_list_modp_ggelu_noneP_kernel(
                     act[:],
                     MULT,
                 )
-            h_c = ring.tile([P, CHUNK], U32, name="h_c", align_bytes=64)
-            h_s = ring.tile([P, CHUNK], U8, name="h_s", align_bytes=64)
+            h_c = held([P, CHUNK], U32, "h_c%d" % c)
+            h_s = held([P, CHUNK], U8, "h_s%d" % c)
             nc.vector.quantize_mx(out=h_c[:].bitcast(FP8X4), scales=h_s[:], in_=h_b[:])
-            tok = slice(c * CHUNK, (c + 1) * CHUNK)
-            for u in range(2):
-                yb = psum.tile([P, 2, CHUNK], F32, name="yb", bufs=3)
-                for e in range(2):
-                    t = 2 * u + e
-                    nc.tensor.matmul_mx(
-                        out=yb[:, e, :],
-                        lhsT=codes[2][:, P * t : P * (t + 1)].bitcast(FP8X4),
-                        lhsT_scale=scales[2][:, P * t : P * (t + 1)],
-                        rhs=h_c[:].bitcast(FP8X4),
-                        rhs_scale=h_s[:],
-                        start=True,
-                        stop=True,
-                    )
-                if u == 0:
-                    y_early = ring.tile([P, 2, CHUNK], F32, name="y_early")
-                    nc.scalar.copy(y_early[:], yb[:])
-                    for e in range(2):
-                        nc.vector.tensor_tensor(
-                            windows[e][:].indirect(offsets[:, c * CHUNK // 16 : (c + 1) * CHUNK // 16]),
-                            y_early[:, e, :],
-                            gate[:, tok],
-                            MULT,
-                        )
-                else:
-                    nc.scalar.copy(y_late[:, :, tok], yb[:])
+            return h_c, h_s
+
+        def down(h_q, u, dst):
+            yb = psum.tile([P, 2, CHUNK], F32, name="yb", bufs=3)
+            for e in range(2):
+                w_codes, w_scales = stationary(wd_q, 2 * u + e)
+                nc.tensor.matmul_mx(
+                    out=yb[:, e, :],
+                    lhsT=w_codes,
+                    lhsT_scale=w_scales,
+                    rhs=h_q[0][:].bitcast(FP8X4),
+                    rhs_scale=h_q[1][:],
+                    start=True,
+                    stop=True,
+                )
+            nc.scalar.copy(dst, yb[:])
+
+        def place_early(c):
+            y_early = ring.tile([P, 2, CHUNK], F32, name="y_early")
+            down(h_q[c], 0, y_early[:])
+            for e in range(2):
+                nc.vector.tensor_tensor(
+                    windows[e][:].indirect(offsets[:, c * CHUNK // 16 : (c + 1) * CHUNK // 16]),
+                    y_early[:, e, :],
+                    gate[:, c * CHUNK : (c + 1) * CHUNK],
+                    MULT,
+                )
+
+        n_chunks = J // CHUNK
+        h_q = [hidden(0)]
+        wd_q = [quantise_half(wd_raw, 0, nc.scalar.copy, "wd0")]
+        for c in range(1, n_chunks):
+            h_q.append(hidden(c))
+            place_early(c - 1)
+        place_early(n_chunks - 1)
+
+        wd_q.append(quantise_half(wd_raw, 1, nc.scalar.copy, "wd1"))
+        for t, tag in ((2, "wd1_grouped"), (3, "h_c0")):
+            if t == 3:
+                y_late = held([P, 2, J], F32, "y_late")
+                for c in range(n_chunks):
+                    down(h_q[c], 1, y_late[:, :, c * CHUNK : (c + 1) * CHUNK])
+            windows.append(held([P, T], F32, "window%d" % t, tag))
+            nc.gpsimd.memset(windows[t][:], 0.0)
 
         rows = out_0.rearrange("(p t) c -> t p c", t=PACK)
-        n_out = T // OUT_CHUNK
-        pairs = [held([P, 2, OUT_CHUNK, 2], BF16, "pairs%d" % o) for o in range(n_out)]
+        n_out = len(OUT_WIDTHS)
+        out_cols = [slice(sum(OUT_WIDTHS[:o]), sum(OUT_WIDTHS[: o + 1])) for o in range(n_out)]
+        pairs = [held([P, 2, OUT_WIDTHS[o], 2], BF16, "pairs%d" % o) for o in range(n_out)]
         for t in range(PACK):
             if t >= 2:
                 nc.vector.tensor_tensor(windows[t][:].indirect(offsets[:]), y_late[:, t - 2, :], gate[:], MULT)
             nc.sync.dma_start(rows[t], windows[t][:])
             for o in range(n_out):
-                nc.scalar.copy(pairs[o][:, t // 2, :, t % 2], windows[t][:, o * OUT_CHUNK : (o + 1) * OUT_CHUNK])
+                copy = nc.vector.tensor_copy if (t >= 2 and o == 0) else nc.scalar.copy
+                copy(pairs[o][:, t // 2, :, t % 2], windows[t][:, out_cols[o]])
 
         out_s = held([P, T], U8, "out_s")
         for o in range(n_out):
-            ocols = slice(o * OUT_CHUNK, (o + 1) * OUT_CHUNK)
-            fin = held([P, OUT_CHUNK * PACK], BF16, "fin%d" % o)
-            nc.vector.tensor_copy(
-                fin[:].bitcast(I32).rearrange("p (c u) -> p c u", u=2),
-                pairs[o][:].rearrange("p u c e -> p u (c e)").bitcast(I32).rearrange("p u c -> p c u"),
+            fin = held([P, OUT_WIDTHS[o] * PACK], BF16, "fin%d" % o)
+            copy, word = (nc.scalar.copy, U32) if o == n_out - 1 else (nc.vector.tensor_copy, I32)
+            copy(
+                fin[:].bitcast(word).rearrange("p (c u) -> p c u", u=2),
+                pairs[o][:].rearrange("p u c e -> p u (c e)").bitcast(word).rearrange("p u c -> p c u"),
             )
-            out_c = held([P, OUT_CHUNK], U32, "out_c%d" % o)
-            nc.vector.quantize_mx(out=out_c[:].bitcast(FP8X4), scales=out_s[:, ocols], in_=fin[:])
+            out_c = held([P, OUT_WIDTHS[o]], U32, "out_c%d" % o)
+            nc.vector.quantize_mx(out=out_c[:].bitcast(FP8X4), scales=out_s[:, out_cols[o]], in_=fin[:])
             nc.sync.dma_start(
-                out_1[0].rearrange("p t b -> p (t b)").bitcast(I32)[:, ocols], out_c[:].bitcast(I32)
+                out_1[0].rearrange("p t b -> p (t b)").bitcast(I32)[:, out_cols[o]], out_c[:].bitcast(I32)
             )
         for q in range(4):
             (nc.sync if q % 2 else nc.scalar).dma_start(

@@ -69,40 +69,58 @@ def tile_list_modp_ggelu_noneP_kernel(
         tok_s = held([P, PASSES, J], U8, "tok_s")
         nc.vector.memset(tok_s[:].rearrange("p a j -> p (a j)").bitcast(I32), 0)
 
+        windows = [held([P, T], F32, "window0")]
+        nc.vector.memset(windows[0][:], 0.0)
+
         picked_s = held([P, J], U8, "picked_s")
         nc.vector.tensor_copy(picked_s[:], tab_s[:].indirect(offsets[:]))
         wu1_raw = load_rows(wu[512:1024, :], "wu1_raw", "tab_s")
         for a in range(PASSES):
             for q in range(4):
-                (nc.gpsimd if q == 3 else nc.sync).dma_start(
+                (nc.gpsimd if (a, q) == (0, 0) else nc.sync).dma_start(
                     tok_s[32 * q : 32 * q + 4, a, :].bitcast(I32),
                     picked_s[16 * a + 4 * q : 16 * a + 4 * q + 4, :].bitcast(I32),
                 )
-        windows = [held([P, T], F32, "window0", "warm")]
-        nc.gpsimd.memset(windows[0][:], 0.0)
 
         tok_w = []
-        for c in range(J // CHUNK):
-            both = held([P, CHUNK], U32, "both%d" % c)
-            nc.vector.tensor_copy(both[:], tab_w[:].indirect(offsets[:, c * CHUNK // 16 : (c + 1) * CHUNK // 16]))
-            parted = held([P, PASSES, 2 * CHUNK], U8, "tok_w%d" % c)
+
+        def pick_words(first, count, tag):
+            width = count * CHUNK
+            both = held([P, width], U32, "both%d" % first, tag)
+            nc.vector.tensor_copy(
+                both[:], tab_w[:].indirect(offsets[:, first * CHUNK // 16 : (first + count) * CHUNK // 16])
+            )
+            parted = held([P, PASSES, 2 * width], U8, "tok_w%d" % first)
             nc.vector.tensor_copy(
                 parted[:].bitcast(U16), both[:].bitcast(U16).rearrange("p (j a) -> p a j", a=PASSES)
             )
-            tok_w.append(parted)
-            if c == 0:
-                wg_w = held([P, PASSES, 2 * R], U8, "wg_w")
-                nc.vector.tensor_copy(
-                    wg_w[:].bitcast(U16).rearrange("p a (t m) -> p a t m", t=PACK),
-                    wg_raw[:].bitcast(U16).rearrange("p a (m t) -> p a t m", t=PACK),
-                )
-                wg_s = held([P, PASSES, R], U8, "wg_s")
-                nc.vector.tensor_copy(
-                    wg_s[:].rearrange("p a (t m) -> p a t m", t=PACK),
-                    wgs_raw[:].rearrange("p a (m t) -> p a t m", t=PACK),
-                )
+            tok_w.extend(parted[:, :, 2 * CHUNK * i : 2 * CHUNK * (i + 1)] for i in range(count))
+
+        pick_words(0, 1, None)
+        wg_w = held([P, PASSES, 2 * R], U8, "wg_w")
+        nc.vector.tensor_copy(
+            wg_w[:].bitcast(U16).rearrange("p a (t m) -> p a t m", t=PACK),
+            wg_raw[:].bitcast(U16).rearrange("p a (m t) -> p a t m", t=PACK),
+        )
+        wg_s = held([P, PASSES, R], U8, "wg_s")
+        nc.vector.tensor_copy(
+            wg_s[:].rearrange("p a (t m) -> p a t m", t=PACK),
+            wgs_raw[:].rearrange("p a (m t) -> p a t m", t=PACK),
+        )
+        pick_words(1, 1, "wgs_raw")
+        spin = psum.tile([P, 2, CHUNK], F32, name="spin", tag="yb", bufs=3)
+        for i in range(3):
+            nc.tensor.matmul_mx(
+                out=spin[:].rearrange("p e j -> p (e j)"),
+                lhsT=wg_w[:, 0, 0 : 2 * P].bitcast(FP4X4),
+                lhsT_scale=wg_s[:, 0, 0:P],
+                rhs=wg_w[:, 0, :].bitcast(FP4X4),
+                rhs_scale=wg_s[:, 0, :],
+                start=True,
+                stop=True,
+            )
         wd_raw = load_rows(wd, "wd_raw", "both0")
-        gate = held([P, J], F32, "gate", "both1")
+        gate = held([P, J], F32, "gate", "wgs_raw")
         nc.sync.dma_start(gate[:], wgo)
 
         def quantise_half(raw, u, copy, name):
@@ -120,8 +138,7 @@ def tile_list_modp_ggelu_noneP_kernel(
             [quantise_half(wu0_raw, 0, nc.scalar.copy, "wu00"), quantise_half(wu0_raw, 1, nc.scalar.copy, "wu01")],
             [quantise_half(wu1_raw, 0, nc.scalar.copy, "wu10"), quantise_half(wu1_raw, 1, nc.vector.tensor_copy, "wu11")],
         ]
-        windows.append(held([P, T], F32, "window1", "wu11_grouped"))
-        nc.vector.memset(windows[1][:], 0.0)
+        pick_words(2, 2, "wu10_grouped")
 
         def stationary(halves, t):
             cod, sca = halves[t // 2]
@@ -129,7 +146,7 @@ def tile_list_modp_ggelu_noneP_kernel(
             return cod[:, cols].bitcast(FP8X4), sca[:, cols]
 
         def hidden(c):
-            h_b = ring.tile([P, CHUNK * PACK], BF16, name="h_b", align_bytes=64)
+            h_b = held([P, CHUNK * PACK], BF16, "h_b%d" % c)
             for s in range(CHUNK // SUB):
                 scale_cols = slice(c * CHUNK + s * SUB, c * CHUNK + (s + 1) * SUB)
                 wcols = slice(2 * s * SUB, 2 * (s + 1) * SUB)
@@ -169,6 +186,9 @@ def tile_list_modp_ggelu_noneP_kernel(
             h_c = held([P, CHUNK], U32, "h_c%d" % c)
             h_s = held([P, CHUNK], U8, "h_s%d" % c)
             nc.vector.quantize_mx(out=h_c[:].bitcast(FP8X4), scales=h_s[:], in_=h_b[:])
+            if c > 0:
+                windows.append(held([P, T], F32, "window%d" % c, "h_b%d" % c))
+                nc.gpsimd.memset(windows[c][:], 0.0)
             return h_c, h_s
 
         def down(h_q, u, dst):
@@ -186,33 +206,32 @@ def tile_list_modp_ggelu_noneP_kernel(
                 )
             nc.scalar.copy(dst, yb[:])
 
-        def place_early(c):
-            y_early = ring.tile([P, 2, CHUNK], F32, name="y_early")
-            down(h_q[c], 0, y_early[:])
-            for e in range(2):
-                nc.vector.tensor_tensor(
-                    windows[e][:].indirect(offsets[:, c * CHUNK // 16 : (c + 1) * CHUNK // 16]),
-                    y_early[:, e, :],
-                    gate[:, c * CHUNK : (c + 1) * CHUNK],
-                    MULT,
-                )
+        def place(c, t):
+            nc.vector.tensor_tensor(
+                windows[t][:].indirect(offsets[:, c * CHUNK // 16 : (c + 1) * CHUNK // 16]),
+                y_early[c][:, t, :],
+                gate[:, c * CHUNK : (c + 1) * CHUNK],
+                MULT,
+            )
 
         n_chunks = J // CHUNK
         h_q = [hidden(0)]
         wd_q = [quantise_half(wd_raw, 0, nc.scalar.copy, "wd0")]
-        for c in range(1, n_chunks):
-            h_q.append(hidden(c))
-            place_early(c - 1)
-        place_early(n_chunks - 1)
+        y_early = []
+        for c in range(n_chunks):
+            if c + 1 < n_chunks:
+                h_q.append(hidden(c + 1))
+            y_early.append(held([P, 2, CHUNK], F32, "y_early%d" % c))
+            down(h_q[c], 0, y_early[c][:])
+            place(c, 0)
+            if c > 0:
+                place(c - 1, 1)
+        place(n_chunks - 1, 1)
 
         wd_q.append(quantise_half(wd_raw, 1, nc.scalar.copy, "wd1"))
-        for t, tag in ((2, "wd1_grouped"), (3, "h_c0")):
-            if t == 3:
-                y_late = held([P, 2, J], F32, "y_late")
-                for c in range(n_chunks):
-                    down(h_q[c], 1, y_late[:, :, c * CHUNK : (c + 1) * CHUNK])
-            windows.append(held([P, T], F32, "window%d" % t, tag))
-            nc.gpsimd.memset(windows[t][:], 0.0)
+        y_late = held([P, 2, J], F32, "y_late")
+        for c in range(n_chunks):
+            down(h_q[c], 1, y_late[:, :, c * CHUNK : (c + 1) * CHUNK])
 
         rows = out_0.rearrange("(p t) c -> t p c", t=PACK)
         n_out = len(OUT_WIDTHS)

@@ -21,7 +21,8 @@ PACK = 4
 PASSES = K // (P * PACK)
 CHUNK = 256
 SUB = 128
-OUT_WIDTHS = (256, 512, 512, 512, 256)
+PAIR_WIDTHS = (512, 512)
+DIRECT_WIDTHS = (512, 256, 256)
 
 
 def tile_list_modp_ggelu_noneP_kernel(
@@ -40,7 +41,7 @@ def tile_list_modp_ggelu_noneP_kernel(
         nc.sync.dma_start(offsets[:], offs)
 
         tab_s = held([P, T], U8, "tab_s")
-        nc.sync.dma_start(tab_s[0:32, :].bitcast(I32), tab_scales.rearrange("a q t -> (a q) t").bitcast(I32))
+        nc.sync.dma_start(tab_s[96:128, :].bitcast(I32), tab_scales.rearrange("a q t -> (a q) t").bitcast(I32))
         tab_w = held([P, T], U32, "tab_w")
         nc.sync.dma_start(tab_w[:].bitcast(I32), tab_words[0].rearrange("p t b -> p (t b)").bitcast(I32))
         wg_raw = held([P, PASSES, 2 * R], U8, "wg_raw")
@@ -60,8 +61,7 @@ def tile_list_modp_ggelu_noneP_kernel(
                 wgs_raw[32 * q : 32 * q + 4, :, :].bitcast(I32),
                 wg_scales[:, 4 * q : 4 * q + 4, :].rearrange("a r c -> r a c").bitcast(I32),
             )
-        nc.vector.memset(tab_s[32:64, :].bitcast(I32), 0)
-        nc.vector.memset(tab_s[64:128, :].bitcast(I32), 0)
+        nc.vector.memset(tab_s[0:96, :].bitcast(I32), 0)
         warm = held([P, 8], F32, "warm")
         warm2 = held([P, 8], F32, "warm2")
         nc.vector.memset(warm[:], 0.0)
@@ -79,7 +79,7 @@ def tile_list_modp_ggelu_noneP_kernel(
             for q in range(4):
                 (nc.gpsimd if (a, q) == (0, 0) else nc.sync).dma_start(
                     tok_s[32 * q : 32 * q + 4, a, :].bitcast(I32),
-                    picked_s[16 * a + 4 * q : 16 * a + 4 * q + 4, :].bitcast(I32),
+                    picked_s[96 + 16 * a + 4 * q : 96 + 16 * a + 4 * q + 4, :].bitcast(I32),
                 )
 
         tok_w = []
@@ -99,13 +99,13 @@ def tile_list_modp_ggelu_noneP_kernel(
         pick_words(0, 1, None)
         wg_w = held([P, PASSES, 2 * R], U8, "wg_w")
         nc.vector.tensor_copy(
-            wg_w[:].bitcast(U16).rearrange("p a (t m) -> p a t m", t=PACK),
-            wg_raw[:].bitcast(U16).rearrange("p a (m t) -> p a t m", t=PACK),
+            wg_w[:].bitcast(I32).rearrange("p a (t q) -> p a q t", t=PACK),
+            wg_raw[:].bitcast(I32).rearrange("p a (q t) -> p a q t", t=PACK),
         )
         wg_s = held([P, PASSES, R], U8, "wg_s")
         nc.vector.tensor_copy(
-            wg_s[:].rearrange("p a (t m) -> p a t m", t=PACK),
-            wgs_raw[:].rearrange("p a (m t) -> p a t m", t=PACK),
+            wg_s[:].bitcast(U16).rearrange("p a (t q) -> p a q t", t=PACK),
+            wgs_raw[:].bitcast(U16).rearrange("p a (q t) -> p a q t", t=PACK),
         )
         pick_words(1, 1, "wgs_raw")
         spin = psum.tile([P, 2, CHUNK], F32, name="spin", tag="yb", bufs=3)
@@ -119,15 +119,17 @@ def tile_list_modp_ggelu_noneP_kernel(
                 start=True,
                 stop=True,
             )
-        wd_raw = load_rows(wd, "wd_raw", "both0")
+        wd_raw = held([P, PACK, N], F32, "wd_raw", "both0")
+        for e in range(2):
+            nc.sync.dma_start(wd_raw[e:P:2, :, :], wd.rearrange("(q t e) n -> e q t n", t=PACK, e=2)[e])
         gate = held([P, J], F32, "gate", "wgs_raw")
         nc.sync.dma_start(gate[:], wgo)
 
-        def quantise_half(raw, u, copy, name):
+        def quantise_half(raw, u, copy, name, e=1):
             grouped = held([P, 2 * P * PACK], BF16, name + "_grouped")
             copy(
-                grouped[:].rearrange("p (t m j) -> p m j t", t=2, j=PACK),
-                raw[:].rearrange("p j (m t) -> p m j t", t=PACK)[:, :, :, 2 * u : 2 * u + 2],
+                grouped[:].rearrange("p (t q e j) -> p q j t e", t=2, e=e, j=PACK),
+                raw[:].rearrange("p j (q t e) -> p q j t e", t=PACK, e=e)[:, :, :, 2 * u : 2 * u + 2, :],
             )
             cod = held([P, 2 * P], U32, name + "_codes")
             sca = held([P, 2 * P], U8, name + "_scales")
@@ -135,8 +137,11 @@ def tile_list_modp_ggelu_noneP_kernel(
             return cod, sca
 
         wu_q = [
-            [quantise_half(wu0_raw, 0, nc.scalar.copy, "wu00"), quantise_half(wu0_raw, 1, nc.scalar.copy, "wu01")],
-            [quantise_half(wu1_raw, 0, nc.scalar.copy, "wu10"), quantise_half(wu1_raw, 1, nc.vector.tensor_copy, "wu11")],
+            [quantise_half(wu0_raw, u, nc.scalar.copy, "wu0%d" % u, 2) for u in range(2)],
+            [
+                quantise_half(wu1_raw, 0, nc.scalar.copy, "wu10", 2),
+                quantise_half(wu1_raw, 1, nc.vector.tensor_copy, "wu11", 2),
+            ],
         ]
         pick_words(2, 2, "wu10_grouped")
 
@@ -186,9 +191,6 @@ def tile_list_modp_ggelu_noneP_kernel(
             h_c = held([P, CHUNK], U32, "h_c%d" % c)
             h_s = held([P, CHUNK], U8, "h_s%d" % c)
             nc.vector.quantize_mx(out=h_c[:].bitcast(FP8X4), scales=h_s[:], in_=h_b[:])
-            if c > 0:
-                windows.append(held([P, T], F32, "window%d" % c, "h_b%d" % c))
-                nc.gpsimd.memset(windows[c][:], 0.0)
             return h_c, h_s
 
         def down(h_q, u, dst):
@@ -206,59 +208,76 @@ def tile_list_modp_ggelu_noneP_kernel(
                 )
             nc.scalar.copy(dst, yb[:])
 
-        def place(c, t):
+        n_chunks = J // CHUNK
+        y = held([P, PACK, J], F32, "y")
+
+        def down_chunk(c, u):
+            down(h_q[c], u, y[:, 2 * u : 2 * u + 2, c * CHUNK : (c + 1) * CHUNK])
+
+        def place(c):
             nc.vector.tensor_tensor(
-                windows[t][:].indirect(offsets[:, c * CHUNK // 16 : (c + 1) * CHUNK // 16]),
-                y_early[c][:, t, :],
+                windows[0][:].indirect(offsets[:, c * CHUNK // 16 : (c + 1) * CHUNK // 16]),
+                y[:, 0, c * CHUNK : (c + 1) * CHUNK],
                 gate[:, c * CHUNK : (c + 1) * CHUNK],
                 MULT,
             )
 
-        n_chunks = J // CHUNK
         h_q = [hidden(0)]
         wd_q = [quantise_half(wd_raw, 0, nc.scalar.copy, "wd0")]
-        y_early = []
         for c in range(n_chunks):
             if c + 1 < n_chunks:
                 h_q.append(hidden(c + 1))
-            y_early.append(held([P, 2, CHUNK], F32, "y_early%d" % c))
-            down(h_q[c], 0, y_early[c][:])
-            place(c, 0)
-            if c > 0:
-                place(c - 1, 1)
-        place(n_chunks - 1, 1)
-
-        wd_q.append(quantise_half(wd_raw, 1, nc.scalar.copy, "wd1"))
-        y_late = held([P, 2, J], F32, "y_late")
-        for c in range(n_chunks):
-            down(h_q[c], 1, y_late[:, :, c * CHUNK : (c + 1) * CHUNK])
+            down_chunk(c, 0)
+            place(c)
+            if c == 0:
+                wd_q.append(quantise_half(wd_raw, 1, nc.scalar.copy, "wd1"))
+            else:
+                down_chunk(c - 1, 1)
+        down_chunk(n_chunks - 1, 1)
+        windows.append(held([P, T], F32, "window1", "h_b%d" % (n_chunks - 1)))
+        nc.gpsimd.memset(windows[1][:], 0.0)
 
         rows = out_0.rearrange("(p t) c -> t p c", t=PACK)
-        n_out = len(OUT_WIDTHS)
-        out_cols = [slice(sum(OUT_WIDTHS[:o]), sum(OUT_WIDTHS[: o + 1])) for o in range(n_out)]
-        pairs = [held([P, 2, OUT_WIDTHS[o], 2], BF16, "pairs%d" % o) for o in range(n_out)]
+        widths = PAIR_WIDTHS + DIRECT_WIDTHS
+        n_pair = len(PAIR_WIDTHS)
+        out_cols = [slice(sum(widths[:o]), sum(widths[: o + 1])) for o in range(len(widths))]
+        pairs = [held([P, 2, w, 2], BF16, "pairs%d" % o) for o, w in enumerate(PAIR_WIDTHS)]
+        fin = [held([P, w, PACK], BF16, "fin%d" % o) for o, w in enumerate(widths)]
         for t in range(PACK):
-            if t >= 2:
-                nc.vector.tensor_tensor(windows[t][:].indirect(offsets[:]), y_late[:, t - 2, :], gate[:], MULT)
-            nc.sync.dma_start(rows[t], windows[t][:])
-            for o in range(n_out):
-                copy = nc.vector.tensor_copy if (t >= 2 and o == 0) else nc.scalar.copy
-                copy(pairs[o][:, t // 2, :, t % 2], windows[t][:, out_cols[o]])
+            window = windows[t % 2]
+            if t > 0:
+                nc.vector.tensor_tensor(window[:].indirect(offsets[:]), y[:, t, :], gate[:], MULT)
+            nc.sync.dma_start(rows[t], window[:])
+            for o, w in enumerate(widths):
+                src = window[:, out_cols[o]]
+                if o >= n_pair:
+                    nc.scalar.copy(fin[o][:, :, t], src)
+                elif t < 2:
+                    nc.scalar.copy(pairs[o][:, 0, :, t], src)
+                elif t == 2:
+                    nc.scalar.copy(pairs[o][:, 1, :, :], src.unsqueeze(2).to_broadcast([P, w, 2]))
+                else:
+                    nc.vector.tensor_copy(pairs[o][:, 1, :, 1], src)
 
-        out_s = held([P, T], U8, "out_s")
-        for o in range(n_out):
-            fin = held([P, OUT_WIDTHS[o] * PACK], BF16, "fin%d" % o)
-            copy, word = (nc.scalar.copy, U32) if o == n_out - 1 else (nc.vector.tensor_copy, I32)
-            copy(
-                fin[:].bitcast(word).rearrange("p (c u) -> p c u", u=2),
-                pairs[o][:].rearrange("p u c e -> p u (c e)").bitcast(word).rearrange("p u c -> p c u"),
+        for o in range(n_pair):
+            nc.vector.tensor_copy(
+                fin[o][:].rearrange("p c t -> p (c t)").bitcast(I32).rearrange("p (c u) -> p c u", u=2),
+                pairs[o][:].rearrange("p u c e -> p u (c e)").bitcast(I32).rearrange("p u c -> p c u"),
             )
-            out_c = held([P, OUT_WIDTHS[o]], U32, "out_c%d" % o)
-            nc.vector.quantize_mx(out=out_c[:].bitcast(FP8X4), scales=out_s[:, out_cols[o]], in_=fin[:])
+        out_s = held([P, T], U8, "out_s")
+
+        def store_scales(cols, queues):
+            for q in range(4):
+                queues[q % len(queues)].dma_start(
+                    out_2[0, 4 * q : 4 * q + 4, cols].bitcast(I32), out_s[32 * q : 32 * q + 4, cols].bitcast(I32)
+                )
+
+        for o, w in enumerate(widths):
+            out_c = held([P, w], U32, "out_c%d" % o)
+            nc.vector.quantize_mx(
+                out=out_c[:].bitcast(FP8X4), scales=out_s[:, out_cols[o]], in_=fin[o][:].rearrange("p c t -> p (c t)")
+            )
             nc.sync.dma_start(
                 out_1[0].rearrange("p t b -> p (t b)").bitcast(I32)[:, out_cols[o]], out_c[:].bitcast(I32)
             )
-        for q in range(4):
-            (nc.sync if q % 2 else nc.scalar).dma_start(
-                out_2[0, 4 * q : 4 * q + 4, :].bitcast(I32), out_s[32 * q : 32 * q + 4, :].bitcast(I32)
-            )
+        store_scales(slice(0, T), [nc.scalar, nc.sync])

@@ -19,8 +19,10 @@ GELU = mybir.ActivationFunctionType.Gelu_apprx_tanh
 P = 128
 PACK = 4
 PASSES = K // (P * PACK)
+HALF = 512
 CHUNK = 256
 SUB = 128
+MOVES_ON_GPSIMD = 2
 PAIR_WIDTHS = (512, 512)
 DIRECT_WIDTHS = (512, 256, 256)
 
@@ -37,205 +39,242 @@ def tile_list_modp_ggelu_noneP_kernel(
         def held(shape, dtype, name, tag=None):
             return keep.tile(shape, dtype, name=name, tag=tag or name, align_bytes=64)
 
+        def entries(first, count):
+            return offsets[:, first // 16 : (first + count) // 16]
+
         offsets = keep.tile([P, J // 16], U16, name="offsets")
         nc.sync.dma_start(offsets[:], offs)
-
         tab_s = held([P, T], U8, "tab_s")
         nc.sync.dma_start(tab_s[96:128, :].bitcast(I32), tab_scales.rearrange("a q t -> (a q) t").bitcast(I32))
         tab_w = held([P, T], U32, "tab_w")
         nc.sync.dma_start(tab_w[:].bitcast(I32), tab_words[0].rearrange("p t b -> p (t b)").bitcast(I32))
         wg_raw = held([P, PASSES, 2 * R], U8, "wg_raw")
         nc.sync.dma_start(wg_raw[:].bitcast(I32), wg_words.rearrange("a p c -> p a c").bitcast(I32))
+        wu_raw = []
+        for a in range(PASSES):
+            for h in range(2):
+                raw = held([P, PACK, R // 2], F32, "wu_raw%d%d" % (a, h))
+                nc.sync.dma_start(
+                    raw[:],
+                    wu[512 * a : 512 * (a + 1), 256 * h : 256 * (h + 1)].rearrange("(p j) c -> p j c", j=PACK),
+                )
+                wu_raw.append(raw)
 
-        def load_rows(src, name, tag=None):
-            raw = held([P, PACK, 512], F32, name, tag)
-            nc.sync.dma_start(raw[:], src.rearrange("(p j) c -> p j c", j=PACK))
-            return raw
-
-        wu0_raw = load_rows(wu[0:512, :], "wu0_raw")
-
+        nc.vector.memset(tab_s[0:96, :].bitcast(I32), 0)
         wgs_raw = held([P, PASSES, R], U8, "wgs_raw")
-        nc.vector.memset(wgs_raw[:].rearrange("p a c -> p (a c)").bitcast(I32), 0)
+        nc.gpsimd.memset(wgs_raw[:].rearrange("p a c -> p (a c)").bitcast(I32), 0)
         for q in range(4):
             nc.scalar.dma_start(
                 wgs_raw[32 * q : 32 * q + 4, :, :].bitcast(I32),
                 wg_scales[:, 4 * q : 4 * q + 4, :].rearrange("a r c -> r a c").bitcast(I32),
             )
-        nc.vector.memset(tab_s[0:96, :].bitcast(I32), 0)
         warm = held([P, 8], F32, "warm")
         warm2 = held([P, 8], F32, "warm2")
         nc.vector.memset(warm[:], 0.0)
         nc.scalar.activation(warm2[:], warm[:], GELU)
         tok_s = held([P, PASSES, J], U8, "tok_s")
-        nc.vector.memset(tok_s[:].rearrange("p a j -> p (a j)").bitcast(I32), 0)
-
-        windows = [held([P, T], F32, "window0")]
-        nc.vector.memset(windows[0][:], 0.0)
+        nc.gpsimd.memset(tok_s[:].rearrange("p a j -> p (a j)").bitcast(I32), 0)
+        windows = [held([P, T], F32, "window%d" % i) for i in range(2)]
+        for window in windows:
+            nc.gpsimd.memset(window[:], 0.0)
 
         picked_s = held([P, J], U8, "picked_s")
         nc.vector.tensor_copy(picked_s[:], tab_s[:].indirect(offsets[:]))
-        wu1_raw = load_rows(wu[512:1024, :], "wu1_raw", "tab_s")
-        for a in range(PASSES):
-            for q in range(4):
-                (nc.gpsimd if (a, q) == (0, 0) else nc.sync).dma_start(
-                    tok_s[32 * q : 32 * q + 4, a, :].bitcast(I32),
-                    picked_s[96 + 16 * a + 4 * q : 96 + 16 * a + 4 * q + 4, :].bitcast(I32),
-                )
+        for m in range(PASSES * 4):
+            a, q = divmod(m, 4)
+            (nc.gpsimd if m < MOVES_ON_GPSIMD else nc.sync).dma_start(
+                tok_s[32 * q : 32 * q + 4, a, :].bitcast(I32),
+                picked_s[96 + 4 * m : 96 + 4 * m + 4, :].bitcast(I32),
+            )
+        wd_raw = held([P, PACK, N], F32, "wd_raw", "tab_s")
+        for e in range(2):
+            nc.sync.dma_start(wd_raw[e:P:2, :, :], wd.rearrange("(q t e) n -> e q t n", t=PACK, e=2)[e])
+        gate = held([P, J], F32, "gate", "picked_s")
+        nc.sync.dma_start(gate[:], wgo)
 
+        both = []
+        for h in range(2):
+            picked_w = held([P, HALF], U32, "picked_w%d" % h)
+            nc.vector.tensor_copy(picked_w[:], tab_w[:].indirect(entries(h * HALF, HALF)))
+            both.append(picked_w)
         tok_w = []
-
-        def pick_words(first, count, tag):
-            width = count * CHUNK
-            both = held([P, width], U32, "both%d" % first, tag)
+        for h in range(2):
+            parted = held([P, PASSES, 2 * HALF], U8, "tok_w%d" % h)
             nc.vector.tensor_copy(
-                both[:], tab_w[:].indirect(offsets[:, first * CHUNK // 16 : (first + count) * CHUNK // 16])
+                parted[:].bitcast(U16), both[h][:].bitcast(U16).rearrange("p (j a) -> p a j", a=PASSES)
             )
-            parted = held([P, PASSES, 2 * width], U8, "tok_w%d" % first)
-            nc.vector.tensor_copy(
-                parted[:].bitcast(U16), both[:].bitcast(U16).rearrange("p (j a) -> p a j", a=PASSES)
-            )
-            tok_w.extend(parted[:, :, 2 * CHUNK * i : 2 * CHUNK * (i + 1)] for i in range(count))
+            tok_w.append(parted)
 
-        pick_words(0, 1, None)
         wg_w = held([P, PASSES, 2 * R], U8, "wg_w")
-        nc.vector.tensor_copy(
-            wg_w[:].bitcast(I32).rearrange("p a (t q) -> p a q t", t=PACK),
-            wg_raw[:].bitcast(I32).rearrange("p a (q t) -> p a q t", t=PACK),
+        nc.scalar.copy(
+            wg_w[:].bitcast(U32).rearrange("p a (t q) -> p a q t", t=PACK),
+            wg_raw[:].bitcast(U32).rearrange("p a (q t) -> p a q t", t=PACK),
         )
         wg_s = held([P, PASSES, R], U8, "wg_s")
-        nc.vector.tensor_copy(
+        nc.scalar.copy(
             wg_s[:].bitcast(U16).rearrange("p a (t q) -> p a q t", t=PACK),
             wgs_raw[:].bitcast(U16).rearrange("p a (q t) -> p a q t", t=PACK),
         )
-        pick_words(1, 1, "wgs_raw")
-        spin = psum.tile([P, 2, CHUNK], F32, name="spin", tag="yb", bufs=3)
-        for i in range(3):
-            nc.tensor.matmul_mx(
-                out=spin[:].rearrange("p e j -> p (e j)"),
-                lhsT=wg_w[:, 0, 0 : 2 * P].bitcast(FP4X4),
-                lhsT_scale=wg_s[:, 0, 0:P],
-                rhs=wg_w[:, 0, :].bitcast(FP4X4),
-                rhs_scale=wg_s[:, 0, :],
-                start=True,
-                stop=True,
-            )
-        wd_raw = held([P, PACK, N], F32, "wd_raw", "both0")
-        for e in range(2):
-            nc.sync.dma_start(wd_raw[e:P:2, :, :], wd.rearrange("(q t e) n -> e q t n", t=PACK, e=2)[e])
-        gate = held([P, J], F32, "gate", "wgs_raw")
-        nc.sync.dma_start(gate[:], wgo)
 
-        def quantise_half(raw, u, copy, name, e=1):
-            grouped = held([P, 2 * P * PACK], BF16, name + "_grouped")
-            copy(
-                grouped[:].rearrange("p (t q e j) -> p q j t e", t=2, e=e, j=PACK),
-                raw[:].rearrange("p j (q t e) -> p q j t e", t=PACK, e=e)[:, :, :, 2 * u : 2 * u + 2, :],
-            )
+        def quantised(grouped, name):
             cod = held([P, 2 * P], U32, name + "_codes")
             sca = held([P, 2 * P], U8, name + "_scales")
             nc.vector.quantize_mx(out=cod[:].bitcast(FP8X4), scales=sca[:], in_=grouped[:])
             return cod, sca
 
-        wu_q = [
-            [quantise_half(wu0_raw, u, nc.scalar.copy, "wu0%d" % u, 2) for u in range(2)],
-            [
-                quantise_half(wu1_raw, 0, nc.scalar.copy, "wu10", 2),
-                quantise_half(wu1_raw, 1, nc.vector.tensor_copy, "wu11", 2),
-            ],
-        ]
-        pick_words(2, 2, "wu10_grouped")
+        wu_q = []
+        for a in range(PASSES):
+            grouped = [held([P, 2 * P * PACK], BF16, "wu_grouped%d%d" % (a, u)) for u in range(2)]
+            for h in range(2):
+                for u in range(2):
+                    last = (a, h, u) == (PASSES - 1, 1, 1)
+                    (nc.vector.tensor_copy if last else nc.scalar.copy)(
+                        grouped[u][:].rearrange("p (t h q e j) -> p h q j t e", t=2, h=2, e=2, j=PACK)[:, h],
+                        wu_raw[2 * a + h][:].rearrange("p j (q t e) -> p q j t e", t=PACK, e=2)[
+                            :, :, :, 2 * u : 2 * u + 2, :
+                        ],
+                    )
+            order = (0, 1) if a == 0 else (1, 0)
+            made = {u: quantised(grouped[u], "wu%d%d" % (a, u)) for u in order}
+            wu_q.append([made[0], made[1]])
+
+        spin = psum.tile([P, HALF], F32, name="spin", tag="yb", bufs=3)
+        for i in range(3):
+            nc.tensor.matmul_mx(
+                out=spin[:],
+                lhsT=wu_q[0][0][0][:, 0:P].bitcast(FP8X4),
+                lhsT_scale=wu_q[0][0][1][:, 0:P],
+                rhs=wg_w[:, 0, :].bitcast(FP4X4),
+                rhs_scale=wg_s[:, 0, :],
+                start=True,
+                stop=True,
+            )
+
+        def round_wd(u, tag):
+            grouped = held([P, 2 * P * PACK], BF16, "wd_grouped%d" % u, tag)
+            nc.scalar.copy(
+                grouped[:].rearrange("p (t q j) -> p q j t", t=2, j=PACK),
+                wd_raw[:].rearrange("p j (q t) -> p q j t", t=PACK)[:, :, :, 2 * u : 2 * u + 2],
+            )
+            return grouped
 
         def stationary(halves, t):
             cod, sca = halves[t // 2]
             cols = slice(P * (t % 2), P * (t % 2 + 1))
             return cod[:, cols].bitcast(FP8X4), sca[:, cols]
 
-        def hidden(c):
-            h_b = held([P, CHUNK * PACK], BF16, "h_b%d" % c)
-            for s in range(CHUNK // SUB):
-                scale_cols = slice(c * CHUNK + s * SUB, c * CHUNK + (s + 1) * SUB)
-                wcols = slice(2 * s * SUB, 2 * (s + 1) * SUB)
-                ga = psum.tile([P, PACK, SUB], F32, name="ga", bufs=2)
-                ub = psum.tile([P, PACK, SUB], F32, name="ub", bufs=3)
-                for t in range(PACK):
-                    for a in range(PASSES):
-                        nc.tensor.matmul_mx(
-                            out=ga[:, t, :],
-                            lhsT=wg_w[:, a, 2 * P * t : 2 * P * (t + 1)].bitcast(FP4X4),
-                            lhsT_scale=wg_s[:, a, P * t : P * (t + 1)],
-                            rhs=tok_w[c][:, a, wcols].bitcast(FP4X4),
-                            rhs_scale=tok_s[:, a, scale_cols],
-                            start=(a == 0),
-                            stop=(a == PASSES - 1),
-                        )
-                act = ring.tile([P, SUB, PACK], F32, name="act")
-                nc.scalar.activation(act[:], ga[:].rearrange("p t j -> p j t"), GELU)
-                for t in range(PACK):
-                    for a in range(PASSES):
-                        w_codes, w_scales = stationary(wu_q[a], t)
-                        nc.tensor.matmul_mx(
-                            out=ub[:, t, :],
-                            lhsT=w_codes,
-                            lhsT_scale=w_scales,
-                            rhs=tok_w[c][:, a, wcols].bitcast(FP4X4),
-                            rhs_scale=tok_s[:, a, scale_cols],
-                            start=(a == 0),
-                            stop=(a == PASSES - 1),
-                        )
-                nc.vector.tensor_tensor(
-                    h_b[:, s * SUB * PACK : (s + 1) * SUB * PACK].rearrange("p (j t) -> p j t", t=PACK),
-                    ub[:].rearrange("p t j -> p j t"),
-                    act[:],
-                    MULT,
-                )
-            h_c = held([P, CHUNK], U32, "h_c%d" % c)
-            h_s = held([P, CHUNK], U8, "h_s%d" % c)
-            nc.vector.quantize_mx(out=h_c[:].bitcast(FP8X4), scales=h_s[:], in_=h_b[:])
-            return h_c, h_s
-
-        def down(h_q, u, dst):
-            yb = psum.tile([P, 2, CHUNK], F32, name="yb", bufs=3)
-            for e in range(2):
-                w_codes, w_scales = stationary(wd_q, 2 * u + e)
-                nc.tensor.matmul_mx(
-                    out=yb[:, e, :],
-                    lhsT=w_codes,
-                    lhsT_scale=w_scales,
-                    rhs=h_q[0][:].bitcast(FP8X4),
-                    rhs_scale=h_q[1][:],
-                    start=True,
-                    stop=True,
-                )
-            nc.scalar.copy(dst, yb[:])
-
         n_chunks = J // CHUNK
-        y = held([P, PACK, J], F32, "y")
+        h_b = [held([P, CHUNK * PACK], BF16, "h_b%d" % c) for c in range(n_chunks)]
+        h_c = held([P, J], U32, "h_c")
+        h_s = held([P, J], U8, "h_s")
+        y = held([P, PACK - 1, J], F32, "y")
+        first_acts = held([P, 2, SUB * PACK], F32, "first_acts", "wu_raw11")
 
-        def down_chunk(c, u):
-            down(h_q[c], u, y[:, 2 * u : 2 * u + 2, c * CHUNK : (c + 1) * CHUNK])
+        last_act = held([P, SUB * PACK], F32, "last_act")
+        y_first = {}
 
-        def place(c):
+        def hidden(s):
+            first = s * SUB
+            words = tok_w[first // HALF][:, :, 2 * (first % HALF) : 2 * (first % HALF + SUB)]
+            ga = psum.tile([P, PACK, SUB], F32, name="ga", bufs=2)
+            ub = psum.tile([P, PACK, SUB], F32, name="ub", bufs=3)
+            for t in range(PACK):
+                for a in range(PASSES):
+                    nc.tensor.matmul_mx(
+                        out=ga[:, t, :],
+                        lhsT=wg_w[:, a, 2 * P * t : 2 * P * (t + 1)].bitcast(FP4X4),
+                        lhsT_scale=wg_s[:, a, P * t : P * (t + 1)],
+                        rhs=words[:, a, :].bitcast(FP4X4),
+                        rhs_scale=tok_s[:, a, first : first + SUB],
+                        start=(a == 0),
+                        stop=(a == PASSES - 1),
+                    )
+            if s < 2:
+                act = first_acts[:, s, :]
+            elif s == J // SUB - 1:
+                act = last_act[:]
+            else:
+                later_act = ring.tile([P, SUB * PACK], F32, name="later_act")
+                act = later_act[:]
+            act = act.rearrange("p (j t) -> p j t", t=PACK)
+            nc.scalar.activation(act, ga[:].rearrange("p t j -> p j t"), GELU)
+            for t in (2, 3, 0, 1):
+                for a in range(PASSES):
+                    w_codes, w_scales = stationary(wu_q[a], t)
+                    nc.tensor.matmul_mx(
+                        out=ub[:, t, :],
+                        lhsT=w_codes,
+                        lhsT_scale=w_scales,
+                        rhs=words[:, a, :].bitcast(FP4X4),
+                        rhs_scale=tok_s[:, a, first : first + SUB],
+                        start=(a == 0),
+                        stop=(a == PASSES - 1),
+                    )
+            lo = (first % CHUNK) * PACK
             nc.vector.tensor_tensor(
-                windows[0][:].indirect(offsets[:, c * CHUNK // 16 : (c + 1) * CHUNK // 16]),
-                y[:, 0, c * CHUNK : (c + 1) * CHUNK],
-                gate[:, c * CHUNK : (c + 1) * CHUNK],
+                h_b[first // CHUNK][:, lo : lo + SUB * PACK].rearrange("p (j t) -> p j t", t=PACK),
+                ub[:].rearrange("p t j -> p j t"),
+                act,
                 MULT,
             )
 
-        h_q = [hidden(0)]
-        wd_q = [quantise_half(wd_raw, 0, nc.scalar.copy, "wd0")]
-        for c in range(n_chunks):
-            if c + 1 < n_chunks:
-                h_q.append(hidden(c + 1))
-            down_chunk(c, 0)
-            place(c)
-            if c == 0:
-                wd_q.append(quantise_half(wd_raw, 1, nc.scalar.copy, "wd1"))
-            else:
-                down_chunk(c - 1, 1)
-        down_chunk(n_chunks - 1, 1)
-        windows.append(held([P, T], F32, "window1", "h_b%d" % (n_chunks - 1)))
-        nc.gpsimd.memset(windows[1][:], 0.0)
+        def quantise_h(c):
+            cols = slice(c * CHUNK, (c + 1) * CHUNK)
+            nc.vector.quantize_mx(out=h_c[:, cols].bitcast(FP8X4), scales=h_s[:, cols], in_=h_b[c][:])
+
+        def down(t, first, count, dst):
+            cols = slice(first, first + count)
+            yb = psum.tile([P, HALF], F32, name="yb", bufs=3)
+            w_codes, w_scales = stationary(wd_q, t)
+            nc.tensor.matmul_mx(
+                out=yb[:, 0:count],
+                lhsT=w_codes,
+                lhsT_scale=w_scales,
+                rhs=h_c[:, cols].bitcast(FP8X4),
+                rhs_scale=h_s[:, cols],
+                start=True,
+                stop=True,
+            )
+            nc.scalar.copy(dst, yb[:, 0:count])
+
+        def place(c):
+            cols = slice(c * CHUNK, (c + 1) * CHUNK)
+            nc.vector.tensor_tensor(
+                windows[0][:].indirect(entries(c * CHUNK, CHUNK)), y_first[c][:], gate[:, cols], MULT
+            )
+
+        def finish(c):
+            quantise_h(c)
+            y_first[c] = held([P, CHUNK], F32, "y_first%d" % c)
+            down(0, c * CHUNK, CHUNK, y_first[c][:])
+
+        hidden(0)
+        hidden(1)
+        wd_q = [quantised(round_wd(0, "wu_grouped10"), "wd0")]
+        finish(0)
+        hidden(2)
+        place(0)
+        hidden(3)
+        finish(1)
+        hidden(4)
+        place(1)
+        hidden(5)
+        hidden(6)
+        quantise_h(2)
+        hidden(7)
+        y_first[2] = held([P, CHUNK], F32, "y_first2", "last_act")
+        down(0, 2 * CHUNK, CHUNK, y_first[2][:])
+        finish(3)
+        place(2)
+        place(3)
+
+        def down_slice(t):
+            for h in range(2):
+                down(t, h * HALF, HALF, y[:, t - 1, h * HALF : (h + 1) * HALF])
+
+        down_slice(1)
+        wd_q.append(quantised(round_wd(1, "h_b%d" % (n_chunks - 1)), "wd1"))
+        down_slice(2)
 
         rows = out_0.rearrange("(p t) c -> t p c", t=PACK)
         widths = PAIR_WIDTHS + DIRECT_WIDTHS
@@ -246,7 +285,7 @@ def tile_list_modp_ggelu_noneP_kernel(
         for t in range(PACK):
             window = windows[t % 2]
             if t > 0:
-                nc.vector.tensor_tensor(window[:].indirect(offsets[:]), y[:, t, :], gate[:], MULT)
+                nc.vector.tensor_tensor(window[:].indirect(offsets[:]), y[:, t - 1, :], gate[:], MULT)
             nc.sync.dma_start(rows[t], window[:])
             for o, w in enumerate(widths):
                 src = window[:, out_cols[o]]
@@ -258,6 +297,8 @@ def tile_list_modp_ggelu_noneP_kernel(
                     nc.scalar.copy(pairs[o][:, 1, :, :], src.unsqueeze(2).to_broadcast([P, w, 2]))
                 else:
                     nc.vector.tensor_copy(pairs[o][:, 1, :, 1], src)
+            if t == 0:
+                down_slice(PACK - 1)
 
         for o in range(n_pair):
             nc.vector.tensor_copy(
@@ -265,13 +306,6 @@ def tile_list_modp_ggelu_noneP_kernel(
                 pairs[o][:].rearrange("p u c e -> p u (c e)").bitcast(I32).rearrange("p u c -> p c u"),
             )
         out_s = held([P, T], U8, "out_s")
-
-        def store_scales(cols, queues):
-            for q in range(4):
-                queues[q % len(queues)].dma_start(
-                    out_2[0, 4 * q : 4 * q + 4, cols].bitcast(I32), out_s[32 * q : 32 * q + 4, cols].bitcast(I32)
-                )
-
         for o, w in enumerate(widths):
             out_c = held([P, w], U32, "out_c%d" % o)
             nc.vector.quantize_mx(
@@ -280,4 +314,7 @@ def tile_list_modp_ggelu_noneP_kernel(
             nc.sync.dma_start(
                 out_1[0].rearrange("p t b -> p (t b)").bitcast(I32)[:, out_cols[o]], out_c[:].bitcast(I32)
             )
-        store_scales(slice(0, T), [nc.scalar, nc.sync])
+        for q in range(4):
+            (nc.scalar, nc.sync)[q % 2].dma_start(
+                out_2[0, 4 * q : 4 * q + 4, :].bitcast(I32), out_s[32 * q : 32 * q + 4, :].bitcast(I32)
+            )

@@ -44,8 +44,8 @@ def tile_list_modp_ggelu_noneP_kernel(
 
         offsets = keep.tile([P, J // 16], U16, name="offsets")
         nc.sync.dma_start(offsets[:], offs)
-        tab_s = held([P, T], U8, "tab_s")
-        nc.sync.dma_start(tab_s[96:128, :].bitcast(I32), tab_scales.rearrange("a q t -> (a q) t").bitcast(I32))
+        tab_s = held([P, T + 4], U8, "tab_s")
+        nc.sync.dma_start(tab_s[96:128, 0:T].bitcast(I32), tab_scales.rearrange("a q t -> (a q) t").bitcast(I32))
         tab_w = held([P, T], U32, "tab_w")
         nc.sync.dma_start(tab_w[:].bitcast(I32), tab_words[0].rearrange("p t b -> p (t b)").bitcast(I32))
         wg_raw = held([P, PASSES, 2 * R], U8, "wg_raw")
@@ -68,18 +68,19 @@ def tile_list_modp_ggelu_noneP_kernel(
                 wgs_raw[32 * q : 32 * q + 4, :, :].bitcast(I32),
                 wg_scales[:, 4 * q : 4 * q + 4, :].rearrange("a r c -> r a c").bitcast(I32),
             )
-        warm = held([P, 8], F32, "warm")
-        warm2 = held([P, 8], F32, "warm2")
+        warm = held([P, 1], F32, "warm")
+        warm2 = held([P, 1], F32, "warm2")
         nc.vector.memset(warm[:], 0.0)
         nc.scalar.activation(warm2[:], warm[:], GELU)
-        tok_s = held([P, PASSES, J], U8, "tok_s")
-        nc.gpsimd.memset(tok_s[:].rearrange("p a j -> p (a j)").bitcast(I32), 0)
+        planes = held([P, PASSES * J + 4], U8, "planes")
+        nc.vector.memset(planes[:].bitcast(I32), 0)
+        tok_s = planes[:, 0 : PASSES * J].rearrange("p (a j) -> p a j", a=PASSES)
         windows = [held([P, T], F32, "window%d" % i) for i in range(2)]
         for window in windows:
             nc.gpsimd.memset(window[:], 0.0)
 
         picked_s = held([P, J], U8, "picked_s")
-        nc.vector.tensor_copy(picked_s[:], tab_s[:].indirect(offsets[:]))
+        nc.vector.tensor_copy(picked_s[:], tab_s[:, 0:T].indirect(offsets[:]))
         for m in range(PASSES * 4):
             a, q = divmod(m, 4)
             (nc.gpsimd if m < MOVES_ON_GPSIMD else nc.sync).dma_start(
@@ -107,13 +108,13 @@ def tile_list_modp_ggelu_noneP_kernel(
 
         wg_w = held([P, PASSES, 2 * R], U8, "wg_w")
         nc.scalar.copy(
-            wg_w[:].bitcast(U32).rearrange("p a (t q) -> p a q t", t=PACK),
-            wg_raw[:].bitcast(U32).rearrange("p a (q t) -> p a q t", t=PACK),
+            wg_w[:].bitcast(U32).rearrange("p a (t g i) -> p a g t i", t=PACK, i=4),
+            wg_raw[:].bitcast(U32).rearrange("p a (g i t) -> p a g t i", t=PACK, i=4),
         )
         wg_s = held([P, PASSES, R], U8, "wg_s")
         nc.scalar.copy(
-            wg_s[:].bitcast(U16).rearrange("p a (t q) -> p a q t", t=PACK),
-            wgs_raw[:].bitcast(U16).rearrange("p a (q t) -> p a q t", t=PACK),
+            wg_s[:].bitcast(U16).rearrange("p a (t g i) -> p a g t i", t=PACK, i=8),
+            wgs_raw[:].bitcast(U16).rearrange("p a (g i t) -> p a g t i", t=PACK, i=8),
         )
 
         def quantised(grouped, name):

@@ -22,7 +22,10 @@ PASSES = K // (P * PACK)
 HALF = 512
 CHUNK = 256
 SUB = 128
-MOVES_ON_GPSIMD = 2
+GATES_AHEAD = 3
+WU_HALF_BYTES = PACK * (R // 2) * 4
+GROUP = 512
+PIECE = 256
 PAIR_WIDTHS = (512, 512)
 DIRECT_WIDTHS = (512, 256, 256)
 
@@ -34,31 +37,40 @@ def tile_list_modp_ggelu_noneP_kernel(
     with ExitStack() as ctx:
         keep = ctx.enter_context(tc.tile_pool(name="keep", bufs=1))
         ring = ctx.enter_context(tc.tile_pool(name="ring", bufs=2))
+        turns = ctx.enter_context(tc.tile_pool(name="turns", bufs=1))
         psum = ctx.enter_context(tc.psum_pool(name="psum", bufs=1))
 
         def held(shape, dtype, name, tag=None):
             return keep.tile(shape, dtype, name=name, tag=tag or name, align_bytes=64)
+
+        def placed(shape, dtype, name, offset):
+            return turns.tile(shape, dtype, name=name, offset=offset, align_bytes=64)
 
         def entries(first, count):
             return offsets[:, first // 16 : (first + count) // 16]
 
         offsets = keep.tile([P, J // 16], U16, name="offsets")
         nc.sync.dma_start(offsets[:], offs)
-        tab_s = held([P, T + 4], U8, "tab_s")
+        tab_s = placed([P, T + 4], U8, "tab_s", WU_HALF_BYTES - T // 2)
         nc.sync.dma_start(tab_s[96:128, 0:T].bitcast(I32), tab_scales.rearrange("a q t -> (a q) t").bitcast(I32))
         tab_w = held([P, T], U32, "tab_w")
         nc.sync.dma_start(tab_w[:].bitcast(I32), tab_words[0].rearrange("p t b -> p (t b)").bitcast(I32))
         wg_raw = held([P, PASSES, 2 * R], U8, "wg_raw")
         nc.sync.dma_start(wg_raw[:].bitcast(I32), wg_words.rearrange("a p c -> p a c").bitcast(I32))
-        wu_raw = []
-        for a in range(PASSES):
-            for h in range(2):
-                raw = held([P, PACK, R // 2], F32, "wu_raw%d%d" % (a, h))
-                nc.sync.dma_start(
-                    raw[:],
-                    wu[512 * a : 512 * (a + 1), 256 * h : 256 * (h + 1)].rearrange("(p j) c -> p j c", j=PACK),
-                )
-                wu_raw.append(raw)
+
+        def load_wu(a, h):
+            name = "wu_raw%d%d" % (a, h)
+            if a == 0:
+                raw = held([P, PACK, R // 2], F32, name)
+            else:
+                raw = placed([P, PACK, R // 2], F32, name, h * WU_HALF_BYTES)
+            nc.sync.dma_start(
+                raw[:],
+                wu[512 * a : 512 * (a + 1), 256 * h : 256 * (h + 1)].rearrange("(p j) c -> p j c", j=PACK),
+            )
+            return raw
+
+        wu_raw = [load_wu(0, 0), load_wu(0, 1)]
 
         nc.vector.memset(tab_s[0:96, :].bitcast(I32), 0)
         wgs_raw = held([P, PASSES, R], U8, "wgs_raw")
@@ -81,17 +93,18 @@ def tile_list_modp_ggelu_noneP_kernel(
 
         picked_s = held([P, J], U8, "picked_s")
         nc.vector.tensor_copy(picked_s[:], tab_s[:, 0:T].indirect(offsets[:]))
-        for m in range(PASSES * 4):
-            a, q = divmod(m, 4)
-            (nc.gpsimd if m < MOVES_ON_GPSIMD else nc.sync).dma_start(
-                tok_s[32 * q : 32 * q + 4, a, :].bitcast(I32),
-                picked_s[96 + 4 * m : 96 + 4 * m + 4, :].bitcast(I32),
-            )
-        wd_raw = held([P, PACK, N], F32, "wd_raw", "tab_s")
-        for e in range(2):
-            nc.sync.dma_start(wd_raw[e:P:2, :, :], wd.rearrange("(q t e) n -> e q t n", t=PACK, e=2)[e])
-        gate = held([P, J], F32, "gate", "picked_s")
-        nc.sync.dma_start(gate[:], wgo)
+
+        def move_plane(a):
+            for q in range(4):
+                row = 96 + 16 * a + 4 * q
+                nc.sync.dma_start(
+                    tok_s[32 * q : 32 * q + 4, a, :].bitcast(I32), picked_s[row : row + 4, :].bitcast(I32)
+                )
+
+        move_plane(0)
+        wu_raw.append(load_wu(1, 0))
+        move_plane(1)
+        wu_raw.append(load_wu(1, 1))
 
         both = []
         for h in range(2):
@@ -105,6 +118,11 @@ def tile_list_modp_ggelu_noneP_kernel(
                 parted[:].bitcast(U16), both[h][:].bitcast(U16).rearrange("p (j a) -> p a j", a=PASSES)
             )
             tok_w.append(parted)
+        wd_raw = held([P, PACK, N], F32, "wd_raw", "tab_w")
+        for e in range(2):
+            nc.sync.dma_start(wd_raw[e:P:2, :, :], wd.rearrange("(q t e) n -> e q t n", t=PACK, e=2)[e])
+        gate = held([P, J], F32, "gate", "picked_w0")
+        nc.sync.dma_start(gate[:], wgo)
 
         wg_w = held([P, PASSES, 2 * R], U8, "wg_w")
         nc.scalar.copy(
@@ -116,6 +134,18 @@ def tile_list_modp_ggelu_noneP_kernel(
             wg_s[:].bitcast(U16).rearrange("p a (t g i) -> p a g t i", t=PACK, i=8),
             wgs_raw[:].bitcast(U16).rearrange("p a (g i t) -> p a g t i", t=PACK, i=8),
         )
+
+        spin = psum.tile([P, HALF], F32, name="spin", tag="yb", bufs=2)
+        for i in range(3):
+            nc.tensor.matmul_mx(
+                out=spin[:],
+                lhsT=wg_w[:, 0, 0 : 2 * P].bitcast(FP4X4),
+                lhsT_scale=wg_s[:, 0, 0:P],
+                rhs=wg_w[:, 0, :].bitcast(FP4X4),
+                rhs_scale=wg_s[:, 0, :],
+                start=True,
+                stop=True,
+            )
 
         def quantised(grouped, name):
             cod = held([P, 2 * P], U32, name + "_codes")
@@ -139,18 +169,6 @@ def tile_list_modp_ggelu_noneP_kernel(
             made = {u: quantised(grouped[u], "wu%d%d" % (a, u)) for u in order}
             wu_q.append([made[0], made[1]])
 
-        spin = psum.tile([P, HALF], F32, name="spin", tag="yb", bufs=3)
-        for i in range(3):
-            nc.tensor.matmul_mx(
-                out=spin[:],
-                lhsT=wu_q[0][0][0][:, 0:P].bitcast(FP8X4),
-                lhsT_scale=wu_q[0][0][1][:, 0:P],
-                rhs=wg_w[:, 0, :].bitcast(FP4X4),
-                rhs_scale=wg_s[:, 0, :],
-                start=True,
-                stop=True,
-            )
-
         def round_wd(u, tag):
             grouped = held([P, 2 * P * PACK], BF16, "wd_grouped%d" % u, tag)
             nc.scalar.copy(
@@ -169,7 +187,7 @@ def tile_list_modp_ggelu_noneP_kernel(
         h_c = held([P, J], U32, "h_c")
         h_s = held([P, J], U8, "h_s")
         y = held([P, PACK - 1, J], F32, "y")
-        first_acts = held([P, 2, SUB * PACK], F32, "first_acts", "wu_raw11")
+        first_acts = placed([P, GATES_AHEAD, SUB * PACK], F32, "first_acts", WU_HALF_BYTES)
 
         last_act = held([P, SUB * PACK], F32, "last_act")
         y_first = {}
@@ -177,20 +195,20 @@ def tile_list_modp_ggelu_noneP_kernel(
         def hidden(s):
             first = s * SUB
             words = tok_w[first // HALF][:, :, 2 * (first % HALF) : 2 * (first % HALF + SUB)]
-            ga = psum.tile([P, PACK, SUB], F32, name="ga", bufs=2)
+            ga = psum.tile([P, PACK, SUB], F32, name="ga", bufs=GATES_AHEAD)
             ub = psum.tile([P, PACK, SUB], F32, name="ub", bufs=3)
-            for t in range(PACK):
-                for a in range(PASSES):
+            for a in range(PASSES):
+                for t in range(PACK):
                     nc.tensor.matmul_mx(
                         out=ga[:, t, :],
                         lhsT=wg_w[:, a, 2 * P * t : 2 * P * (t + 1)].bitcast(FP4X4),
                         lhsT_scale=wg_s[:, a, P * t : P * (t + 1)],
                         rhs=words[:, a, :].bitcast(FP4X4),
                         rhs_scale=tok_s[:, a, first : first + SUB],
-                        start=(a == 0),
-                        stop=(a == PASSES - 1),
+                        start=(a, t) == (0, 0),
+                        stop=(a, t) == (PASSES - 1, PACK - 1),
                     )
-            if s < 2:
+            if s < GATES_AHEAD:
                 act = first_acts[:, s, :]
             elif s == J // SUB - 1:
                 act = last_act[:]
@@ -199,8 +217,8 @@ def tile_list_modp_ggelu_noneP_kernel(
                 act = later_act[:]
             act = act.rearrange("p (j t) -> p j t", t=PACK)
             nc.scalar.activation(act, ga[:].rearrange("p t j -> p j t"), GELU)
-            for t in (2, 3, 0, 1):
-                for a in range(PASSES):
+            for a in range(PASSES):
+                for t in (2, 3, 0, 1):
                     w_codes, w_scales = stationary(wu_q[a], t)
                     nc.tensor.matmul_mx(
                         out=ub[:, t, :],
@@ -208,8 +226,8 @@ def tile_list_modp_ggelu_noneP_kernel(
                         lhsT_scale=w_scales,
                         rhs=words[:, a, :].bitcast(FP4X4),
                         rhs_scale=tok_s[:, a, first : first + SUB],
-                        start=(a == 0),
-                        stop=(a == PASSES - 1),
+                        start=(a, t) == (0, 2),
+                        stop=(a, t) == (PASSES - 1, 1),
                     )
             lo = (first % CHUNK) * PACK
             nc.vector.tensor_tensor(
@@ -225,7 +243,10 @@ def tile_list_modp_ggelu_noneP_kernel(
 
         def down(t, first, count, dst):
             cols = slice(first, first + count)
-            yb = psum.tile([P, HALF], F32, name="yb", bufs=3)
+            if t == 0:
+                yb = psum.tile([P, HALF], F32, name="yb", bufs=2)
+            else:
+                yb = psum.tile([P, HALF], F32, name="late_yb", tag="ub", bufs=3)
             w_codes, w_scales = stationary(wd_q, t)
             nc.tensor.matmul_mx(
                 out=yb[:, 0:count],
@@ -244,18 +265,22 @@ def tile_list_modp_ggelu_noneP_kernel(
                 windows[0][:].indirect(entries(c * CHUNK, CHUNK)), y_first[c][:], gate[:, cols], MULT
             )
 
+        def first_slice(c, tag=None):
+            y_first[c] = held([P, CHUNK], F32, "y_first%d" % c, tag)
+            down(0, c * CHUNK, CHUNK, y_first[c][:])
+
         def finish(c):
             quantise_h(c)
-            y_first[c] = held([P, CHUNK], F32, "y_first%d" % c)
-            down(0, c * CHUNK, CHUNK, y_first[c][:])
+            first_slice(c)
 
         hidden(0)
         hidden(1)
-        wd_q = [quantised(round_wd(0, "wu_grouped10"), "wd0")]
-        finish(0)
+        quantise_h(0)
         hidden(2)
-        place(0)
+        wd_q = [quantised(round_wd(0, "wu_grouped10"), "wd0")]
+        first_slice(0)
         hidden(3)
+        place(0)
         finish(1)
         hidden(4)
         place(1)
@@ -263,8 +288,7 @@ def tile_list_modp_ggelu_noneP_kernel(
         hidden(6)
         quantise_h(2)
         hidden(7)
-        y_first[2] = held([P, CHUNK], F32, "y_first2", "last_act")
-        down(0, 2 * CHUNK, CHUNK, y_first[2][:])
+        first_slice(2, "last_act")
         finish(3)
         place(2)
         place(3)
@@ -306,16 +330,21 @@ def tile_list_modp_ggelu_noneP_kernel(
                 fin[o][:].rearrange("p c t -> p (c t)").bitcast(I32).rearrange("p (c u) -> p c u", u=2),
                 pairs[o][:].rearrange("p u c e -> p u (c e)").bitcast(I32).rearrange("p u c -> p c u"),
             )
-        out_s = held([P, T], U8, "out_s")
+        out_s = held([P, GROUP], U8, "out_s")
         for o, w in enumerate(widths):
             out_c = held([P, w], U32, "out_c%d" % o)
-            nc.vector.quantize_mx(
-                out=out_c[:].bitcast(FP8X4), scales=out_s[:, out_cols[o]], in_=fin[o][:].rearrange("p c t -> p (c t)")
-            )
+            for lo in range(0, w, PIECE):
+                group, col = divmod(out_cols[o].start + lo, GROUP)
+                nc.vector.quantize_mx(
+                    out=out_c[:, lo : lo + PIECE].bitcast(FP8X4),
+                    scales=out_s[4 * group : P, col : col + PIECE],
+                    in_=fin[o][:, lo : lo + PIECE, :].rearrange("p c t -> p (c t)"),
+                )
             nc.sync.dma_start(
                 out_1[0].rearrange("p t b -> p (t b)").bitcast(I32)[:, out_cols[o]], out_c[:].bitcast(I32)
             )
         for q in range(4):
             (nc.scalar, nc.sync)[q % 2].dma_start(
-                out_2[0, 4 * q : 4 * q + 4, :].bitcast(I32), out_s[32 * q : 32 * q + 4, :].bitcast(I32)
+                out_2[0, 4 * q : 4 * q + 4, :].bitcast(I32).rearrange("r (g c) -> g r c", g=T // GROUP),
+                out_s[32 * q : 32 * q + 16, :].bitcast(I32),
             )

@@ -119,8 +119,8 @@ def tile_list_modp_ggelu_noneP_kernel(
             )
             tok_w.append(parted)
         wd_raw = held([P, PACK, N], F32, "wd_raw", "tab_w")
-        for e in range(2):
-            nc.sync.dma_start(wd_raw[e:P:2, :, :], wd.rearrange("(q t e) n -> e q t n", t=PACK, e=2)[e])
+        for t in range(PACK):
+            nc.sync.dma_start(wd_raw[:, t, :], wd.rearrange("(q t e) n -> t q e n", t=PACK, e=2)[t])
         gate = held([P, J], F32, "gate", "picked_w0")
         nc.sync.dma_start(gate[:], wgo)
 

@@ -23,7 +23,6 @@ HALF = 512
 CHUNK = 256
 SUB = 128
 GATES_AHEAD = 3
-WU_HALF_BYTES = PACK * (R // 2) * 4
 GROUP = 512
 PIECE = 256
 PAIR_WIDTHS = (512, 512)
@@ -37,40 +36,29 @@ def tile_list_modp_ggelu_noneP_kernel(
     with ExitStack() as ctx:
         keep = ctx.enter_context(tc.tile_pool(name="keep", bufs=1))
         ring = ctx.enter_context(tc.tile_pool(name="ring", bufs=2))
-        turns = ctx.enter_context(tc.tile_pool(name="turns", bufs=1))
         psum = ctx.enter_context(tc.psum_pool(name="psum", bufs=1))
 
         def held(shape, dtype, name, tag=None):
             return keep.tile(shape, dtype, name=name, tag=tag or name, align_bytes=64)
-
-        def placed(shape, dtype, name, offset):
-            return turns.tile(shape, dtype, name=name, offset=offset, align_bytes=64)
 
         def entries(first, count):
             return offsets[:, first // 16 : (first + count) // 16]
 
         offsets = keep.tile([P, J // 16], U16, name="offsets")
         nc.sync.dma_start(offsets[:], offs)
-        tab_s = placed([P, T + 4], U8, "tab_s", WU_HALF_BYTES - T // 2)
+        tab_s = held([P, T + 4], U8, "tab_s")
         nc.sync.dma_start(tab_s[96:128, 0:T].bitcast(I32), tab_scales.rearrange("a q t -> (a q) t").bitcast(I32))
         tab_w = held([P, T], U32, "tab_w")
         nc.sync.dma_start(tab_w[:].bitcast(I32), tab_words[0].rearrange("p t b -> p (t b)").bitcast(I32))
         wg_raw = held([P, PASSES, 2 * R], U8, "wg_raw")
         nc.sync.dma_start(wg_raw[:].bitcast(I32), wg_words.rearrange("a p c -> p a c").bitcast(I32))
 
-        def load_wu(a, h):
-            name = "wu_raw%d%d" % (a, h)
-            if a == 0:
-                raw = held([P, PACK, R // 2], F32, name)
-            else:
-                raw = placed([P, PACK, R // 2], F32, name, h * WU_HALF_BYTES)
-            nc.sync.dma_start(
-                raw[:],
-                wu[512 * a : 512 * (a + 1), 256 * h : 256 * (h + 1)].rearrange("(p j) c -> p j c", j=PACK),
-            )
+        def load_wu(a, tag):
+            raw = held([P, PACK, R], F32, "wu_raw%d" % a, tag)
+            nc.sync.dma_start(raw[:], wu[512 * a : 512 * (a + 1), :].rearrange("(p j) c -> p j c", j=PACK))
             return raw
 
-        wu_raw = [load_wu(0, 0), load_wu(0, 1)]
+        wu_raw = [load_wu(0, None)]
 
         nc.vector.memset(tab_s[0:96, :].bitcast(I32), 0)
         wgs_raw = held([P, PASSES, R], U8, "wgs_raw")
@@ -102,9 +90,8 @@ def tile_list_modp_ggelu_noneP_kernel(
                 )
 
         move_plane(0)
-        wu_raw.append(load_wu(1, 0))
+        wu_raw.append(load_wu(1, "tab_s"))
         move_plane(1)
-        wu_raw.append(load_wu(1, 1))
 
         both = []
         for h in range(2):
@@ -156,16 +143,12 @@ def tile_list_modp_ggelu_noneP_kernel(
         wu_q = []
         for a in range(PASSES):
             grouped = [held([P, 2 * P * PACK], BF16, "wu_grouped%d%d" % (a, u)) for u in range(2)]
-            for h in range(2):
-                for u in range(2):
-                    last = (a, h, u) == (PASSES - 1, 1, 1)
-                    (nc.vector.tensor_copy if last else nc.scalar.copy)(
-                        grouped[u][:].rearrange("p (t h q e j) -> p h q j t e", t=2, h=2, e=2, j=PACK)[:, h],
-                        wu_raw[2 * a + h][:].rearrange("p j (q t e) -> p q j t e", t=PACK, e=2)[
-                            :, :, :, 2 * u : 2 * u + 2, :
-                        ],
-                    )
-            order = (0, 1) if a == 0 else (1, 0)
+            for u, copy in enumerate((nc.scalar.copy, nc.vector.tensor_copy)):
+                copy(
+                    grouped[u][:].rearrange("p (t q e j) -> p q j t e", t=2, e=2, j=PACK),
+                    wu_raw[a][:].rearrange("p j (q t e) -> p q j t e", t=PACK, e=2)[:, :, :, 2 * u : 2 * u + 2, :],
+                )
+            order = (1, 0)
             made = {u: quantised(grouped[u], "wu%d%d" % (a, u)) for u in order}
             wu_q.append([made[0], made[1]])
 
@@ -187,7 +170,7 @@ def tile_list_modp_ggelu_noneP_kernel(
         h_c = held([P, J], U32, "h_c")
         h_s = held([P, J], U8, "h_s")
         y = held([P, PACK - 1, J], F32, "y")
-        first_acts = placed([P, GATES_AHEAD, SUB * PACK], F32, "first_acts", WU_HALF_BYTES)
+        first_acts = held([P, GATES_AHEAD, SUB * PACK], F32, "first_acts", "tab_s")
 
         last_act = held([P, SUB * PACK], F32, "last_act")
         y_first = {}
@@ -281,12 +264,13 @@ def tile_list_modp_ggelu_noneP_kernel(
         first_slice(0)
         hidden(3)
         place(0)
-        finish(1)
+        quantise_h(1)
         hidden(4)
-        place(1)
         hidden(5)
-        hidden(6)
         quantise_h(2)
+        hidden(6)
+        first_slice(1)
+        place(1)
         hidden(7)
         first_slice(2, "last_act")
         finish(3)

@@ -23,6 +23,7 @@ HALF = 512
 CHUNK = 256
 SUB = 128
 GATES_AHEAD = 3
+ROW_PAIR_BYTES = 2 * R * 4
 GROUP = 512
 PIECE = 256
 PAIR_WIDTHS = (512, 512)
@@ -36,29 +37,30 @@ def tile_list_modp_ggelu_noneP_kernel(
     with ExitStack() as ctx:
         keep = ctx.enter_context(tc.tile_pool(name="keep", bufs=1))
         ring = ctx.enter_context(tc.tile_pool(name="ring", bufs=2))
+        turns = ctx.enter_context(tc.tile_pool(name="turns", bufs=1))
         psum = ctx.enter_context(tc.psum_pool(name="psum", bufs=1))
 
         def held(shape, dtype, name, tag=None):
             return keep.tile(shape, dtype, name=name, tag=tag or name, align_bytes=64)
+
+        def placed(shape, dtype, name, offset):
+            return turns.tile(shape, dtype, name=name, offset=offset, align_bytes=64)
 
         def entries(first, count):
             return offsets[:, first // 16 : (first + count) // 16]
 
         offsets = keep.tile([P, J // 16], U16, name="offsets")
         nc.sync.dma_start(offsets[:], offs)
-        tab_s = held([P, T + 4], U8, "tab_s")
+        tab_s = placed([P, T + 4], U8, "tab_s", ROW_PAIR_BYTES - T // 2)
         nc.sync.dma_start(tab_s[96:128, 0:T].bitcast(I32), tab_scales.rearrange("a q t -> (a q) t").bitcast(I32))
         tab_w = held([P, T], U32, "tab_w")
         nc.sync.dma_start(tab_w[:].bitcast(I32), tab_words[0].rearrange("p t b -> p (t b)").bitcast(I32))
         wg_raw = held([P, PASSES, 2 * R], U8, "wg_raw")
         nc.sync.dma_start(wg_raw[:].bitcast(I32), wg_words.rearrange("a p c -> p a c").bitcast(I32))
 
-        def load_wu(a, tag):
-            raw = held([P, PACK, R], F32, "wu_raw%d" % a, tag)
-            nc.sync.dma_start(raw[:], wu[512 * a : 512 * (a + 1), :].rearrange("(p j) c -> p j c", j=PACK))
-            return raw
-
-        wu_raw = [load_wu(0, None)]
+        wu_rows = wu.rearrange("(a p j) c -> a p j c", a=PASSES, j=PACK)
+        wu_first = held([P, PACK, R], F32, "wu_first")
+        nc.sync.dma_start(wu_first[:], wu_rows[0])
 
         nc.vector.memset(tab_s[0:96, :].bitcast(I32), 0)
         wgs_raw = held([P, PASSES, R], U8, "wgs_raw")
@@ -72,9 +74,8 @@ def tile_list_modp_ggelu_noneP_kernel(
         warm2 = held([P, 1], F32, "warm2")
         nc.vector.memset(warm[:], 0.0)
         nc.scalar.activation(warm2[:], warm[:], GELU)
-        planes = held([P, PASSES * J + 4], U8, "planes")
-        nc.vector.memset(planes[:].bitcast(I32), 0)
-        tok_s = planes[:, 0 : PASSES * J].rearrange("p (a j) -> p a j", a=PASSES)
+        tok_s = held([P, PASSES, J], U8, "tok_s")
+        nc.gpsimd.memset(tok_s[:].rearrange("p a j -> p (a j)").bitcast(I32), 0)
         windows = [held([P, T], F32, "window%d" % i) for i in range(2)]
         for window in windows:
             nc.gpsimd.memset(window[:], 0.0)
@@ -90,7 +91,11 @@ def tile_list_modp_ggelu_noneP_kernel(
                 )
 
         move_plane(0)
-        wu_raw.append(load_wu(1, "tab_s"))
+        wu_second = []
+        for i in range(2):
+            raw = placed([P, 2, R], F32, "wu_second%d" % i, i * ROW_PAIR_BYTES)
+            nc.sync.dma_start(raw[:], wu_rows[1][:, 2 * i : 2 * i + 2, :])
+            wu_second.append(raw)
         move_plane(1)
 
         both = []
@@ -140,17 +145,21 @@ def tile_list_modp_ggelu_noneP_kernel(
             nc.vector.quantize_mx(out=cod[:].bitcast(FP8X4), scales=sca[:], in_=grouped[:])
             return cod, sca
 
-        wu_q = []
-        for a in range(PASSES):
-            grouped = [held([P, 2 * P * PACK], BF16, "wu_grouped%d%d" % (a, u)) for u in range(2)]
+        def round_wu(copy, grouped, raw, u, rows, cols):
+            copy(
+                grouped[:].rearrange("p (t q e j) -> p q j t e", t=2, e=2, j=PACK)[:, cols, rows],
+                raw[:].rearrange("p j (q t e) -> p q j t e", t=PACK, e=2)[:, cols, :, 2 * u : 2 * u + 2, :],
+            )
+
+        grouped = [[held([P, 2 * P * PACK], BF16, "wu_grouped%d%d" % (a, u)) for u in range(2)] for a in range(PASSES)]
+        round_wu(nc.scalar.copy, grouped[0][0], wu_first, 0, slice(0, 4), slice(0, 64))
+        round_wu(nc.scalar.copy, grouped[0][1], wu_first, 1, slice(0, 4), slice(0, 32))
+        round_wu(nc.vector.tensor_copy, grouped[0][1], wu_first, 1, slice(0, 4), slice(32, 64))
+        wu_q = [[quantised(grouped[0][u], "wu0%d" % u) for u in range(2)]]
+        for i in range(2):
             for u, copy in enumerate((nc.scalar.copy, nc.vector.tensor_copy)):
-                copy(
-                    grouped[u][:].rearrange("p (t q e j) -> p q j t e", t=2, e=2, j=PACK),
-                    wu_raw[a][:].rearrange("p j (q t e) -> p q j t e", t=PACK, e=2)[:, :, :, 2 * u : 2 * u + 2, :],
-                )
-            order = (1, 0)
-            made = {u: quantised(grouped[u], "wu%d%d" % (a, u)) for u in order}
-            wu_q.append([made[0], made[1]])
+                round_wu(copy, grouped[1][u], wu_second[i], u, slice(2 * i, 2 * i + 2), slice(0, 64))
+        wu_q.append([quantised(grouped[1][u], "wu1%d" % u) for u in (1, 0)][::-1])
 
         def round_wd(u, tag):
             grouped = held([P, 2 * P * PACK], BF16, "wd_grouped%d" % u, tag)
@@ -170,7 +179,7 @@ def tile_list_modp_ggelu_noneP_kernel(
         h_c = held([P, J], U32, "h_c")
         h_s = held([P, J], U8, "h_s")
         y = held([P, PACK - 1, J], F32, "y")
-        first_acts = held([P, GATES_AHEAD, SUB * PACK], F32, "first_acts", "tab_s")
+        first_acts = placed([P, GATES_AHEAD, SUB * PACK], F32, "first_acts", ROW_PAIR_BYTES)
 
         last_act = held([P, SUB * PACK], F32, "last_act")
         y_first = {}
@@ -198,8 +207,8 @@ def tile_list_modp_ggelu_noneP_kernel(
             else:
                 later_act = ring.tile([P, SUB * PACK], F32, name="later_act")
                 act = later_act[:]
-            act = act.rearrange("p (j t) -> p j t", t=PACK)
-            nc.scalar.activation(act, ga[:].rearrange("p t j -> p j t"), GELU)
+            act = act.rearrange("p (g i t) -> p g t i", t=PACK, i=2)
+            nc.scalar.activation(act, ga[:].rearrange("p t (g i) -> p g t i", i=2), GELU)
             for a in range(PASSES):
                 for t in (2, 3, 0, 1):
                     w_codes, w_scales = stationary(wu_q[a], t)
@@ -214,8 +223,8 @@ def tile_list_modp_ggelu_noneP_kernel(
                     )
             lo = (first % CHUNK) * PACK
             nc.vector.tensor_tensor(
-                h_b[first // CHUNK][:, lo : lo + SUB * PACK].rearrange("p (j t) -> p j t", t=PACK),
-                ub[:].rearrange("p t j -> p j t"),
+                h_b[first // CHUNK][:, lo : lo + SUB * PACK].rearrange("p (g i t) -> p g t i", t=PACK, i=2),
+                ub[:].rearrange("p t (g i) -> p g t i", i=2),
                 act,
                 MULT,
             )

@@ -24,6 +24,8 @@ CHUNK = 256
 SUB = 128
 GATES_AHEAD = 3
 ROW_PAIR_BYTES = 2 * R * 4
+SECOND_H = 3 * ROW_PAIR_BYTES
+GPSIMD_STAGES = (4, 5)
 GROUP = 512
 PIECE = 256
 PAIR_WIDTHS = (512, 512)
@@ -175,7 +177,8 @@ def tile_list_modp_ggelu_noneP_kernel(
             return cod[:, cols].bitcast(FP8X4), sca[:, cols]
 
         n_chunks = J // CHUNK
-        h_b = [held([P, CHUNK * PACK], BF16, "h_b%d" % c) for c in range(n_chunks)]
+        h_b = {c: held([P, CHUNK * PACK], BF16, "h_b%d" % c) for c in (0, n_chunks - 1)}
+        h_b[1] = placed([P, CHUNK * PACK], BF16, "h_b1", SECOND_H)
         h_c = held([P, J], U32, "h_c")
         h_s = held([P, J], U8, "h_s")
         y = held([P, PACK - 1, J], F32, "y")
@@ -207,6 +210,7 @@ def tile_list_modp_ggelu_noneP_kernel(
             else:
                 later_act = ring.tile([P, SUB * PACK], F32, name="later_act")
                 act = later_act[:]
+            flat_act = act
             act = act.rearrange("p (g i t) -> p g t i", t=PACK, i=2)
             nc.scalar.activation(act, ga[:].rearrange("p t (g i) -> p g t i", i=2), GELU)
             for a in range(PASSES):
@@ -222,18 +226,20 @@ def tile_list_modp_ggelu_noneP_kernel(
                         stop=(a, t) == (PASSES - 1, 1),
                     )
             lo = (first % CHUNK) * PACK
-            nc.vector.tensor_tensor(
-                h_b[first // CHUNK][:, lo : lo + SUB * PACK].rearrange("p (g i t) -> p g t i", t=PACK, i=2),
-                ub[:].rearrange("p t (g i) -> p g t i", i=2),
-                act,
-                MULT,
-            )
+            dst = h_b[first // CHUNK][:, lo : lo + SUB * PACK]
+            sums = ub[:].rearrange("p t (g i) -> p g t i", i=2)
+            if s in GPSIMD_STAGES:
+                up = held([P, SUB * PACK], F32, "up%d" % s)
+                nc.scalar.copy(up[:].rearrange("p (g i t) -> p g t i", t=PACK, i=2), sums)
+                nc.gpsimd.tensor_tensor(dst, up[:], flat_act, MULT)
+            else:
+                nc.vector.tensor_tensor(dst.rearrange("p (g i t) -> p g t i", t=PACK, i=2), sums, act, MULT)
 
         def quantise_h(c):
             cols = slice(c * CHUNK, (c + 1) * CHUNK)
             nc.vector.quantize_mx(out=h_c[:, cols].bitcast(FP8X4), scales=h_s[:, cols], in_=h_b[c][:])
 
-        def down(t, first, count, dst):
+        def down(t, first, count):
             cols = slice(first, first + count)
             if t == 0:
                 yb = psum.tile([P, HALF], F32, name="yb", bufs=2)
@@ -249,7 +255,7 @@ def tile_list_modp_ggelu_noneP_kernel(
                 start=True,
                 stop=True,
             )
-            nc.scalar.copy(dst, yb[:, 0:count])
+            return yb[:, 0:count]
 
         def place(c):
             cols = slice(c * CHUNK, (c + 1) * CHUNK)
@@ -259,7 +265,7 @@ def tile_list_modp_ggelu_noneP_kernel(
 
         def first_slice(c, tag=None):
             y_first[c] = held([P, CHUNK], F32, "y_first%d" % c, tag)
-            down(0, c * CHUNK, CHUNK, y_first[c][:])
+            nc.scalar.copy(y_first[c][:], down(0, c * CHUNK, CHUNK))
 
         def finish(c):
             quantise_h(c)
@@ -270,15 +276,18 @@ def tile_list_modp_ggelu_noneP_kernel(
         quantise_h(0)
         hidden(2)
         wd_q = [quantised(round_wd(0, "wu_grouped10"), "wd0")]
-        first_slice(0)
+        first_sums = down(0, 0, CHUNK)
         hidden(3)
-        place(0)
         quantise_h(1)
+        weighted = placed([P, CHUNK], F32, "weighted", SECOND_H + CHUNK * 4)
+        nc.vector.tensor_tensor(weighted[:], first_sums, gate[:, 0:CHUNK], MULT)
+        nc.vector.tensor_copy(windows[0][:].indirect(entries(0, CHUNK)), weighted[:])
+        h_b[2] = placed([P, CHUNK * PACK], BF16, "h_b2", SECOND_H - CHUNK * 4)
         hidden(4)
         hidden(5)
-        quantise_h(2)
         hidden(6)
-        first_slice(1)
+        quantise_h(2)
+        first_slice(1, "up%d" % GPSIMD_STAGES[-1])
         place(1)
         hidden(7)
         first_slice(2, "last_act")
@@ -288,7 +297,7 @@ def tile_list_modp_ggelu_noneP_kernel(
 
         def down_slice(t):
             for h in range(2):
-                down(t, h * HALF, HALF, y[:, t - 1, h * HALF : (h + 1) * HALF])
+                nc.scalar.copy(y[:, t - 1, h * HALF : (h + 1) * HALF], down(t, h * HALF, HALF))
 
         down_slice(1)
         wd_q.append(quantised(round_wd(1, "h_b%d" % (n_chunks - 1)), "wd1"))

@@ -53,8 +53,8 @@ def tile_list_modp_ggelu_noneP_kernel(
 
         offsets = keep.tile([P, J // 16], U16, name="offsets")
         nc.sync.dma_start(offsets[:], offs)
-        tab_s = placed([P, T + 4], U8, "tab_s", ROW_PAIR_BYTES - T // 2)
-        nc.sync.dma_start(tab_s[96:128, 0:T].bitcast(I32), tab_scales.rearrange("a q t -> (a q) t").bitcast(I32))
+        tab_s = placed([P, T], U8, "tab_s", ROW_PAIR_BYTES - T // 2)
+        nc.sync.dma_start(tab_s[96:128, :].bitcast(I32), tab_scales.rearrange("a q t -> (a q) t").bitcast(I32))
         tab_w = held([P, T], U32, "tab_w")
         nc.sync.dma_start(tab_w[:].bitcast(I32), tab_words[0].rearrange("p t b -> p (t b)").bitcast(I32))
         wg_raw = held([P, PASSES, 2 * R], U8, "wg_raw")
@@ -64,7 +64,8 @@ def tile_list_modp_ggelu_noneP_kernel(
         wu_first = held([P, PACK, R], F32, "wu_first")
         nc.sync.dma_start(wu_first[:], wu_rows[0])
 
-        nc.vector.memset(tab_s[0:96, :].bitcast(I32), 0)
+        nc.vector.memset(tab_s[0:96, 0 : T - 4].bitcast(I32), 0)
+        nc.vector.memset(tab_s[0:96, T - 4 : T].bitcast(I32), 0)
         wgs_raw = held([P, PASSES, R], U8, "wgs_raw")
         nc.gpsimd.memset(wgs_raw[:].rearrange("p a c -> p (a c)").bitcast(I32), 0)
         for q in range(4):
@@ -83,7 +84,7 @@ def tile_list_modp_ggelu_noneP_kernel(
             nc.gpsimd.memset(window[:], 0.0)
 
         picked_s = held([P, J], U8, "picked_s")
-        nc.vector.tensor_copy(picked_s[:], tab_s[:, 0:T].indirect(offsets[:]))
+        nc.vector.tensor_copy(picked_s[:], tab_s[:].indirect(offsets[:]))
 
         def move_plane(a):
             for q in range(4):
@@ -155,8 +156,8 @@ def tile_list_modp_ggelu_noneP_kernel(
 
         grouped = [[held([P, 2 * P * PACK], BF16, "wu_grouped%d%d" % (a, u)) for u in range(2)] for a in range(PASSES)]
         round_wu(nc.scalar.copy, grouped[0][0], wu_first, 0, slice(0, 4), slice(0, 64))
-        round_wu(nc.scalar.copy, grouped[0][1], wu_first, 1, slice(0, 4), slice(0, 32))
-        round_wu(nc.vector.tensor_copy, grouped[0][1], wu_first, 1, slice(0, 4), slice(32, 64))
+        round_wu(nc.scalar.copy, grouped[0][1], wu_first, 1, slice(0, 4), slice(0, 16))
+        round_wu(nc.vector.tensor_copy, grouped[0][1], wu_first, 1, slice(0, 4), slice(16, 64))
         wu_q = [[quantised(grouped[0][u], "wu0%d" % u) for u in range(2)]]
         for i in range(2):
             for u, copy in enumerate((nc.scalar.copy, nc.vector.tensor_copy)):

@@ -25,6 +25,7 @@ SUB = 128
 GATES_AHEAD = 3
 ROW_PAIR_BYTES = 2 * R * 4
 SECOND_H = 3 * ROW_PAIR_BYTES
+LAST_ROUNDED = 4 * ROW_PAIR_BYTES
 GPSIMD_STAGES = (4, 5)
 GROUP = 512
 PIECE = 256
@@ -107,12 +108,15 @@ def tile_list_modp_ggelu_noneP_kernel(
             nc.vector.tensor_copy(picked_w[:], tab_w[:].indirect(entries(h * HALF, HALF)))
             both.append(picked_w)
         tok_w = []
-        for h in range(2):
-            parted = held([P, PASSES, 2 * HALF], U8, "tok_w%d" % h)
+
+        def part_words(parted):
+            picked = both[len(tok_w)]
             nc.vector.tensor_copy(
-                parted[:].bitcast(U16), both[h][:].bitcast(U16).rearrange("p (j a) -> p a j", a=PASSES)
+                parted[:].bitcast(U16), picked[:].bitcast(U16).rearrange("p (j a) -> p a j", a=PASSES)
             )
             tok_w.append(parted)
+
+        part_words(held([P, PASSES, 2 * HALF], U8, "tok_w0"))
         wd_raw = held([P, PACK, N], F32, "wd_raw", "tab_w")
         for t in range(PACK):
             nc.sync.dma_start(wd_raw[:, t, :], wd.rearrange("(q t e) n -> t q e n", t=PACK, e=2)[t])
@@ -154,18 +158,24 @@ def tile_list_modp_ggelu_noneP_kernel(
                 raw[:].rearrange("p j (q t e) -> p q j t e", t=PACK, e=2)[:, cols, :, 2 * u : 2 * u + 2, :],
             )
 
-        grouped = [[held([P, 2 * P * PACK], BF16, "wu_grouped%d%d" % (a, u)) for u in range(2)] for a in range(PASSES)]
+        grouped = [
+            [held([P, 2 * P * PACK], BF16, "wu_grouped0%d" % u) for u in range(2)],
+            [placed([P, 2 * P * PACK], BF16, "wu_grouped10", LAST_ROUNDED), held([P, 2 * P * PACK], BF16, "wu_grouped11")],
+        ]
         round_wu(nc.scalar.copy, grouped[0][0], wu_first, 0, slice(0, 4), slice(0, 64))
-        round_wu(nc.scalar.copy, grouped[0][1], wu_first, 1, slice(0, 4), slice(0, 16))
-        round_wu(nc.vector.tensor_copy, grouped[0][1], wu_first, 1, slice(0, 4), slice(16, 64))
+        round_wu(nc.vector.tensor_copy, grouped[0][1], wu_first, 1, slice(0, 4), slice(0, 64))
         wu_q = [[quantised(grouped[0][u], "wu0%d" % u) for u in range(2)]]
         for i in range(2):
-            for u, copy in enumerate((nc.scalar.copy, nc.vector.tensor_copy)):
-                round_wu(copy, grouped[1][u], wu_second[i], u, slice(2 * i, 2 * i + 2), slice(0, 64))
+            shared = (64, 32)[i]
+            rows = slice(2 * i, 2 * i + 2)
+            round_wu(nc.scalar.copy, grouped[1][0], wu_second[i], 0, rows, slice(0, shared))
+            round_wu(nc.vector.tensor_copy, grouped[1][1], wu_second[i], 1, rows, slice(0, 64))
+            if shared < 64:
+                round_wu(nc.vector.tensor_copy, grouped[1][0], wu_second[i], 0, rows, slice(shared, 64))
         wu_q.append([quantised(grouped[1][u], "wu1%d" % u) for u in (1, 0)][::-1])
+        part_words(placed([P, PASSES, 2 * HALF], U8, "tok_w1", LAST_ROUNDED + 1024))
 
-        def round_wd(u, tag):
-            grouped = held([P, 2 * P * PACK], BF16, "wd_grouped%d" % u, tag)
+        def round_wd(u, grouped):
             nc.scalar.copy(
                 grouped[:].rearrange("p (t q j) -> p q j t", t=2, j=PACK),
                 wd_raw[:].rearrange("p j (q t) -> p q j t", t=PACK)[:, :, :, 2 * u : 2 * u + 2],
@@ -276,7 +286,7 @@ def tile_list_modp_ggelu_noneP_kernel(
         hidden(1)
         quantise_h(0)
         hidden(2)
-        wd_q = [quantised(round_wd(0, "wu_grouped10"), "wd0")]
+        wd_q = [quantised(round_wd(0, placed([P, 2 * P * PACK], BF16, "wd_grouped0", LAST_ROUNDED - 1024)), "wd0")]
         first_sums = down(0, 0, CHUNK)
         hidden(3)
         quantise_h(1)
@@ -301,7 +311,7 @@ def tile_list_modp_ggelu_noneP_kernel(
                 nc.scalar.copy(y[:, t - 1, h * HALF : (h + 1) * HALF], down(t, h * HALF, HALF))
 
         down_slice(1)
-        wd_q.append(quantised(round_wd(1, "h_b%d" % (n_chunks - 1)), "wd1"))
+        wd_q.append(quantised(round_wd(1, held([P, 2 * P * PACK], BF16, "wd_grouped1", "h_b%d" % (n_chunks - 1))), "wd1"))
         down_slice(2)
 
         rows = out_0.rearrange("(p t) c -> t p c", t=PACK)

@@ -55,7 +55,7 @@ def tile_list_modp_ggelu_noneP_kernel(
         offsets = keep.tile([P, J // 16], U16, name="offsets")
         nc.sync.dma_start(offsets[:], offs)
         tab_s = placed([P, T], U8, "tab_s", ROW_PAIR_BYTES - T // 2)
-        nc.sync.dma_start(tab_s[96:128, :].bitcast(I32), tab_scales.rearrange("a q t -> (a q) t").bitcast(I32))
+        nc.sync.dma_start(tab_s[96:128, :].bitcast(I32), tab_scales.rearrange("a q t -> q a t").bitcast(I32))
         tab_w = held([P, T], U32, "tab_w")
         nc.sync.dma_start(tab_w[:].bitcast(I32), tab_words[0].rearrange("p t b -> p (t b)").bitcast(I32))
         wg_raw = held([P, PASSES, 2 * R], U8, "wg_raw")
@@ -87,20 +87,17 @@ def tile_list_modp_ggelu_noneP_kernel(
         picked_s = held([P, J], U8, "picked_s")
         nc.vector.tensor_copy(picked_s[:], tab_s[:].indirect(offsets[:]))
 
-        def move_plane(a):
-            for q in range(4):
-                row = 96 + 16 * a + 4 * q
-                nc.sync.dma_start(
-                    tok_s[32 * q : 32 * q + 4, a, :].bitcast(I32), picked_s[row : row + 4, :].bitcast(I32)
-                )
-
-        move_plane(0)
+        for q in range(4):
+            row = 96 + 8 * q
+            nc.sync.dma_start(
+                tok_s[32 * q : 32 * q + 4, :, :].rearrange("p a j -> p (a j)").bitcast(I32),
+                picked_s[row : row + 8, :].bitcast(I32),
+            )
         wu_second = []
         for i in range(2):
             raw = placed([P, 2, R], F32, "wu_second%d" % i, i * ROW_PAIR_BYTES)
             nc.sync.dma_start(raw[:], wu_rows[1][:, 2 * i : 2 * i + 2, :])
             wu_second.append(raw)
-        move_plane(1)
 
         both = []
         for h in range(2):

@@ -99,11 +99,7 @@ def tile_list_modp_ggelu_noneP_kernel(
             nc.sync.dma_start(raw[:], wu_rows[1][:, 2 * i : 2 * i + 2, :])
             wu_second.append(raw)
 
-        both = []
-        for h in range(2):
-            picked_w = held([P, HALF], U32, "picked_w%d" % h)
-            nc.vector.tensor_copy(picked_w[:], tab_w[:].indirect(entries(h * HALF, HALF)))
-            both.append(picked_w)
+        both = [held([P, HALF], U32, "picked_w%d" % h) for h in range(2)]
         tok_w = []
 
         def part_words(parted):
@@ -113,7 +109,12 @@ def tile_list_modp_ggelu_noneP_kernel(
             )
             tok_w.append(parted)
 
+        nc.vector.tensor_copy(both[0][:], tab_w[:].indirect(entries(0, HALF)))
         part_words(held([P, PASSES, 2 * HALF], U8, "tok_w0"))
+        for c in range(2):
+            nc.vector.tensor_copy(
+                both[1][:, c * CHUNK : (c + 1) * CHUNK], tab_w[:].indirect(entries(HALF + c * CHUNK, CHUNK))
+            )
         wd_raw = held([P, PACK, N], F32, "wd_raw", "tab_w")
         for t in range(PACK):
             nc.sync.dma_start(wd_raw[:, t, :], wd.rearrange("(q t e) n -> t q e n", t=PACK, e=2)[t])
@@ -157,7 +158,7 @@ def tile_list_modp_ggelu_noneP_kernel(
 
         grouped = [
             [held([P, 2 * P * PACK], BF16, "wu_grouped0%d" % u) for u in range(2)],
-            [placed([P, 2 * P * PACK], BF16, "wu_grouped10", LAST_ROUNDED), held([P, 2 * P * PACK], BF16, "wu_grouped11")],
+            [placed([P, 2 * P * PACK], BF16, "wu_grouped10", LAST_ROUNDED), placed([P, 2 * P * PACK], BF16, "wu_grouped11", LAST_ROUNDED + 2048)],
         ]
         round_wu(nc.scalar.copy, grouped[0][0], wu_first, 0, slice(0, 4), slice(0, 64))
         round_wu(nc.vector.tensor_copy, grouped[0][1], wu_first, 1, slice(0, 4), slice(0, 64))
@@ -170,7 +171,7 @@ def tile_list_modp_ggelu_noneP_kernel(
             if shared < 64:
                 round_wu(nc.vector.tensor_copy, grouped[1][0], wu_second[i], 0, rows, slice(shared, 64))
         wu_q.append([quantised(grouped[1][u], "wu1%d" % u) for u in (1, 0)][::-1])
-        part_words(placed([P, PASSES, 2 * HALF], U8, "tok_w1", LAST_ROUNDED + 1024))
+        part_words(placed([P, PASSES, 2 * HALF], U8, "tok_w1", LAST_ROUNDED + 2048))
 
         def round_wd(u, grouped):
             nc.scalar.copy(
@@ -195,7 +196,7 @@ def tile_list_modp_ggelu_noneP_kernel(
         last_act = held([P, SUB * PACK], F32, "last_act")
         y_first = {}
 
-        def hidden(s):
+        def project(s):
             first = s * SUB
             words = tok_w[first // HALF][:, :, 2 * (first % HALF) : 2 * (first % HALF + SUB)]
             ga = psum.tile([P, PACK, SUB], F32, name="ga", bufs=GATES_AHEAD)
@@ -233,15 +234,23 @@ def tile_list_modp_ggelu_noneP_kernel(
                         start=(a, t) == (0, 2),
                         stop=(a, t) == (PASSES - 1, 1),
                     )
-            lo = (first % CHUNK) * PACK
-            dst = h_b[first // CHUNK][:, lo : lo + SUB * PACK]
             sums = ub[:].rearrange("p t (g i) -> p g t i", i=2)
             if s in GPSIMD_STAGES:
                 up = held([P, SUB * PACK], F32, "up%d" % s)
                 nc.scalar.copy(up[:].rearrange("p (g i t) -> p g t i", t=PACK, i=2), sums)
-                nc.gpsimd.tensor_tensor(dst, up[:], flat_act, MULT)
+                return up[:], flat_act
+            return sums, act
+
+        def multiply(s, factors):
+            lo = (s * SUB % CHUNK) * PACK
+            dst = h_b[s * SUB // CHUNK][:, lo : lo + SUB * PACK]
+            if s in GPSIMD_STAGES:
+                nc.gpsimd.tensor_tensor(dst, *factors, MULT)
             else:
-                nc.vector.tensor_tensor(dst.rearrange("p (g i t) -> p g t i", t=PACK, i=2), sums, act, MULT)
+                nc.vector.tensor_tensor(dst.rearrange("p (g i t) -> p g t i", t=PACK, i=2), *factors, MULT)
+
+        def hidden(s):
+            multiply(s, project(s))
 
         def quantise_h(c):
             cols = slice(c * CHUNK, (c + 1) * CHUNK)
@@ -284,14 +293,15 @@ def tile_list_modp_ggelu_noneP_kernel(
         quantise_h(0)
         hidden(2)
         wd_q = [quantised(round_wd(0, placed([P, 2 * P * PACK], BF16, "wd_grouped0", LAST_ROUNDED - 1024)), "wd0")]
-        first_sums = down(0, 0, CHUNK)
         hidden(3)
+        fifth = project(4)
+        first_sums = down(0, 0, CHUNK)
         quantise_h(1)
         weighted = placed([P, CHUNK], F32, "weighted", SECOND_H + CHUNK * 4)
         nc.vector.tensor_tensor(weighted[:], first_sums, gate[:, 0:CHUNK], MULT)
         nc.vector.tensor_copy(windows[0][:].indirect(entries(0, CHUNK)), weighted[:])
         h_b[2] = placed([P, CHUNK * PACK], BF16, "h_b2", SECOND_H - CHUNK * 4)
-        hidden(4)
+        multiply(4, fifth)
         hidden(5)
         hidden(6)
         quantise_h(2)

@@ -293,12 +293,12 @@ def tile_list_modp_ggelu_noneP_kernel(
         quantise_h(0)
         hidden(2)
         wd_q = [quantised(round_wd(0, placed([P, 2 * P * PACK], BF16, "wd_grouped0", LAST_ROUNDED - 1024)), "wd0")]
+        first_sums = down(0, 0, CHUNK)
         hidden(3)
         fifth = project(4)
-        first_sums = down(0, 0, CHUNK)
-        quantise_h(1)
-        weighted = placed([P, CHUNK], F32, "weighted", SECOND_H + CHUNK * 4)
+        weighted = held([P, CHUNK], F32, "weighted")
         nc.vector.tensor_tensor(weighted[:], first_sums, gate[:, 0:CHUNK], MULT)
+        quantise_h(1)
         nc.vector.tensor_copy(windows[0][:].indirect(entries(0, CHUNK)), weighted[:])
         h_b[2] = placed([P, CHUNK * PACK], BF16, "h_b2", SECOND_H - CHUNK * 4)
         multiply(4, fifth)

@@ -176,7 +176,7 @@ def tile_list_modp_ggelu_noneP_kernel(
         def round_wd(u, grouped):
             nc.scalar.copy(
                 grouped[:].rearrange("p (t q j) -> p q j t", t=2, j=PACK),
-                wd_raw[:].rearrange("p j (q t) -> p q j t", t=PACK)[:, :, :, 2 * u : 2 * u + 2],
+                wd_raw[:].rearrange("p j (q e u) -> p q j e u", e=2, u=2)[:, :, :, :, u],
             )
             return grouped
 
@@ -331,17 +331,16 @@ def tile_list_modp_ggelu_noneP_kernel(
             window = windows[t % 2]
             if t > 0:
                 nc.vector.tensor_tensor(window[:].indirect(offsets[:]), y[:, t - 1, :], gate[:], MULT)
-            nc.sync.dma_start(rows[t], window[:])
-            for o, w in enumerate(widths):
+            slot = 2 * (t % 2) + t // 2
+            nc.sync.dma_start(rows[slot], window[:])
+            for o in range(len(widths)):
                 src = window[:, out_cols[o]]
                 if o >= n_pair:
-                    nc.scalar.copy(fin[o][:, :, t], src)
-                elif t < 2:
-                    nc.scalar.copy(pairs[o][:, 0, :, t], src)
-                elif t == 2:
-                    nc.scalar.copy(pairs[o][:, 1, :, :], src.unsqueeze(2).to_broadcast([P, w, 2]))
+                    nc.scalar.copy(fin[o][:, :, slot], src)
+                elif t < PACK - 1:
+                    nc.scalar.copy(pairs[o][:, slot // 2, :, slot % 2], src)
                 else:
-                    nc.vector.tensor_copy(pairs[o][:, 1, :, 1], src)
+                    nc.vector.tensor_copy(pairs[o][:, slot // 2, :, slot % 2], src)
             if t == 0:
                 down_slice(PACK - 1)
 

@@ -26,6 +26,8 @@ GATES_AHEAD = 3
 ROW_PAIR_BYTES = 2 * R * 4
 SECOND_H = 3 * ROW_PAIR_BYTES
 LAST_ROUNDED = 4 * ROW_PAIR_BYTES
+SLICES = (1, 0, 2, 3)
+LAST_H = 6 * ROW_PAIR_BYTES
 GPSIMD_STAGES = (4, 5)
 GROUP = 512
 PIECE = 256
@@ -79,7 +81,6 @@ def tile_list_modp_ggelu_noneP_kernel(
         nc.vector.memset(warm[:], 0.0)
         nc.scalar.activation(warm2[:], warm[:], GELU)
         tok_s = held([P, PASSES, J], U8, "tok_s")
-        nc.gpsimd.memset(tok_s[:].rearrange("p a j -> p (a j)").bitcast(I32), 0)
         windows = [held([P, T], F32, "window%d" % i) for i in range(2)]
         for window in windows:
             nc.gpsimd.memset(window[:], 0.0)
@@ -132,7 +133,7 @@ def tile_list_modp_ggelu_noneP_kernel(
             wgs_raw[:].bitcast(U16).rearrange("p a (g i t) -> p a g t i", t=PACK, i=8),
         )
 
-        spin = psum.tile([P, HALF], F32, name="spin", tag="yb", bufs=2)
+        spin = psum.tile([P, HALF], F32, name="spin", tag="turn")
         for i in range(3):
             nc.tensor.matmul_mx(
                 out=spin[:],
@@ -186,7 +187,8 @@ def tile_list_modp_ggelu_noneP_kernel(
             return cod[:, cols].bitcast(FP8X4), sca[:, cols]
 
         n_chunks = J // CHUNK
-        h_b = {c: held([P, CHUNK * PACK], BF16, "h_b%d" % c) for c in (0, n_chunks - 1)}
+        h_b = {0: held([P, CHUNK * PACK], BF16, "h_b0")}
+        h_b[n_chunks - 1] = placed([P, CHUNK * PACK], BF16, "h_b3", LAST_H)
         h_b[1] = placed([P, CHUNK * PACK], BF16, "h_b1", SECOND_H)
         h_c = held([P, J], U32, "h_c")
         h_s = held([P, J], U8, "h_s")
@@ -256,13 +258,15 @@ def tile_list_modp_ggelu_noneP_kernel(
             cols = slice(c * CHUNK, (c + 1) * CHUNK)
             nc.vector.quantize_mx(out=h_c[:, cols].bitcast(FP8X4), scales=h_s[:, cols], in_=h_b[c][:])
 
-        def down(t, first, count):
+        def down(t, first, count, tag=None):
             cols = slice(first, first + count)
-            if t == 0:
-                yb = psum.tile([P, HALF], F32, name="yb", bufs=2)
+            if tag:
+                yb = psum.tile([P, HALF], F32, name="yb", tag=tag)
+            elif t == 0:
+                yb = psum.tile([P, HALF], F32, name="yb", bufs=1)
             else:
                 yb = psum.tile([P, HALF], F32, name="late_yb", tag="ub", bufs=3)
-            w_codes, w_scales = stationary(wd_q, t)
+            w_codes, w_scales = stationary(wd_q, SLICES[t])
             nc.tensor.matmul_mx(
                 out=yb[:, 0:count],
                 lhsT=w_codes,
@@ -284,10 +288,6 @@ def tile_list_modp_ggelu_noneP_kernel(
             y_first[c] = held([P, CHUNK], F32, "y_first%d" % c, tag)
             nc.scalar.copy(y_first[c][:], down(0, c * CHUNK, CHUNK))
 
-        def finish(c):
-            quantise_h(c)
-            first_slice(c)
-
         hidden(0)
         hidden(1)
         quantise_h(0)
@@ -308,17 +308,23 @@ def tile_list_modp_ggelu_noneP_kernel(
         first_slice(1, "up%d" % GPSIMD_STAGES[-1])
         place(1)
         hidden(7)
-        first_slice(2, "last_act")
-        finish(3)
+        y_first[2] = held([P, CHUNK], F32, "y_first2")
+        nc.scalar.copy(y_first[2][:], down(0, 2 * CHUNK, CHUNK, "turn"))
         place(2)
+        quantise_h(3)
+        windows.append(placed([P, T], F32, "window2", LAST_H + CHUNK * PACK))
+        nc.gpsimd.memset(windows[2][:], 0.0)
+        nc.scalar.copy(y[:, 0, 0:HALF], down(1, 0, HALF, "turn"))
+        nc.vector.tensor_tensor(windows[1][:].indirect(entries(0, HALF)), y[:, 0, 0:HALF], gate[:, 0:HALF], MULT)
+        first_slice(3)
         place(3)
+        nc.scalar.copy(y[:, 0, HALF:J], down(1, HALF, HALF))
 
         def down_slice(t):
             for h in range(2):
                 nc.scalar.copy(y[:, t - 1, h * HALF : (h + 1) * HALF], down(t, h * HALF, HALF))
 
-        down_slice(1)
-        wd_q.append(quantised(round_wd(1, held([P, 2 * P * PACK], BF16, "wd_grouped1", "h_b%d" % (n_chunks - 1))), "wd1"))
+        wd_q.append(quantised(round_wd(1, placed([P, 2 * P * PACK], BF16, "wd_grouped1", LAST_H - CHUNK * PACK)), "wd1"))
         down_slice(2)
 
         rows = out_0.rearrange("(p t) c -> t p c", t=PACK)
@@ -328,10 +334,12 @@ def tile_list_modp_ggelu_noneP_kernel(
         pairs = [held([P, 2, w, 2], BF16, "pairs%d" % o) for o, w in enumerate(PAIR_WIDTHS)]
         fin = [held([P, w, PACK], BF16, "fin%d" % o) for o, w in enumerate(widths)]
         for t in range(PACK):
-            window = windows[t % 2]
-            if t > 0:
+            window = windows[t % 3]
+            if t == 1:
+                nc.vector.tensor_tensor(window[:].indirect(entries(HALF, HALF)), y[:, 0, HALF:J], gate[:, HALF:J], MULT)
+            elif t > 1:
                 nc.vector.tensor_tensor(window[:].indirect(offsets[:]), y[:, t - 1, :], gate[:], MULT)
-            slot = 2 * (t % 2) + t // 2
+            slot = 2 * (SLICES[t] % 2) + SLICES[t] // 2
             nc.sync.dma_start(rows[slot], window[:])
             for o in range(len(widths)):
                 src = window[:, out_cols[o]]

@@ -27,12 +27,12 @@ ROW_PAIR_BYTES = 2 * R * 4
 SECOND_H = 3 * ROW_PAIR_BYTES
 LAST_ROUNDED = 4 * ROW_PAIR_BYTES
 SLICES = (1, 0, 2, 3)
-LAST_H = 6 * ROW_PAIR_BYTES
-GPSIMD_STAGES = (4, 5)
+LAST_H = SECOND_H + 2048
+GPSIMD_TOKENS = {4: SUB, 5: SUB // 2}
 GROUP = 512
 PIECE = 256
-PAIR_WIDTHS = (512, 512)
-DIRECT_WIDTHS = (512, 256, 256)
+PIECE_WIDTHS = (512, 512, 512, 256, 256)
+PAIRED = (512, 384)
 
 
 def tile_list_modp_ggelu_noneP_kernel(
@@ -186,9 +186,7 @@ def tile_list_modp_ggelu_noneP_kernel(
             cols = slice(P * (t % 2), P * (t % 2 + 1))
             return cod[:, cols].bitcast(FP8X4), sca[:, cols]
 
-        n_chunks = J // CHUNK
         h_b = {0: held([P, CHUNK * PACK], BF16, "h_b0")}
-        h_b[n_chunks - 1] = placed([P, CHUNK * PACK], BF16, "h_b3", LAST_H)
         h_b[1] = placed([P, CHUNK * PACK], BF16, "h_b1", SECOND_H)
         h_c = held([P, J], U32, "h_c")
         h_s = held([P, J], U8, "h_s")
@@ -237,19 +235,25 @@ def tile_list_modp_ggelu_noneP_kernel(
                         stop=(a, t) == (PASSES - 1, 1),
                     )
             sums = ub[:].rearrange("p t (g i) -> p g t i", i=2)
-            if s in GPSIMD_STAGES:
-                up = held([P, SUB * PACK], F32, "up%d" % s)
-                nc.scalar.copy(up[:].rearrange("p (g i t) -> p g t i", t=PACK, i=2), sums)
-                return up[:], flat_act
-            return sums, act
+            share = GPSIMD_TOKENS.get(s, 0)
+            up = None
+            if share:
+                up = held([P, share * PACK], F32, "up%d" % s)
+                nc.scalar.copy(up[:].rearrange("p (g i t) -> p g t i", t=PACK, i=2), sums[:, 0 : share // 2])
+            return sums, act, up, flat_act
 
         def multiply(s, factors):
+            sums, act, up, flat_act = factors
             lo = (s * SUB % CHUNK) * PACK
             dst = h_b[s * SUB // CHUNK][:, lo : lo + SUB * PACK]
-            if s in GPSIMD_STAGES:
-                nc.gpsimd.tensor_tensor(dst, *factors, MULT)
-            else:
-                nc.vector.tensor_tensor(dst.rearrange("p (g i t) -> p g t i", t=PACK, i=2), *factors, MULT)
+            share = GPSIMD_TOKENS.get(s, 0)
+            if share:
+                nc.gpsimd.tensor_tensor(dst[:, 0 : share * PACK], up[:], flat_act[:, 0 : share * PACK], MULT)
+            if share < SUB:
+                rest = slice(share // 2, SUB // 2)
+                nc.vector.tensor_tensor(
+                    dst.rearrange("p (g i t) -> p g t i", t=PACK, i=2)[:, rest], sums[:, rest], act[:, rest], MULT
+                )
 
         def hidden(s):
             multiply(s, project(s))
@@ -303,16 +307,18 @@ def tile_list_modp_ggelu_noneP_kernel(
         h_b[2] = placed([P, CHUNK * PACK], BF16, "h_b2", SECOND_H - CHUNK * 4)
         multiply(4, fifth)
         hidden(5)
+        h_b[3] = placed([P, CHUNK * PACK], BF16, "h_b3", LAST_H)
         hidden(6)
         quantise_h(2)
-        first_slice(1, "up%d" % GPSIMD_STAGES[-1])
+        first_slice(1, "up5")
         place(1)
+        wd_q.append(quantised(round_wd(1, placed([P, 2 * P * PACK], BF16, "wd_grouped1", SECOND_H)), "wd1"))
         hidden(7)
         y_first[2] = held([P, CHUNK], F32, "y_first2")
         nc.scalar.copy(y_first[2][:], down(0, 2 * CHUNK, CHUNK, "turn"))
         place(2)
         quantise_h(3)
-        windows.append(placed([P, T], F32, "window2", LAST_H + CHUNK * PACK))
+        windows.append(placed([P, T], F32, "window2", SECOND_H))
         nc.gpsimd.memset(windows[2][:], 0.0)
         nc.scalar.copy(y[:, 0, 0:HALF], down(1, 0, HALF, "turn"))
         nc.vector.tensor_tensor(windows[1][:].indirect(entries(0, HALF)), y[:, 0, 0:HALF], gate[:, 0:HALF], MULT)
@@ -324,14 +330,13 @@ def tile_list_modp_ggelu_noneP_kernel(
             for h in range(2):
                 nc.scalar.copy(y[:, t - 1, h * HALF : (h + 1) * HALF], down(t, h * HALF, HALF))
 
-        wd_q.append(quantised(round_wd(1, placed([P, 2 * P * PACK], BF16, "wd_grouped1", LAST_H - CHUNK * PACK)), "wd1"))
         down_slice(2)
 
         rows = out_0.rearrange("(p t) c -> t p c", t=PACK)
-        widths = PAIR_WIDTHS + DIRECT_WIDTHS
-        n_pair = len(PAIR_WIDTHS)
+        widths = PIECE_WIDTHS
+        n_pair = len(PAIRED)
         out_cols = [slice(sum(widths[:o]), sum(widths[: o + 1])) for o in range(len(widths))]
-        pairs = [held([P, 2, w, 2], BF16, "pairs%d" % o) for o, w in enumerate(PAIR_WIDTHS)]
+        pairs = [held([P, 2, w, 2], BF16, "pairs%d" % o) for o, w in enumerate(PAIRED)]
         fin = [held([P, w, PACK], BF16, "fin%d" % o) for o, w in enumerate(widths)]
         for t in range(PACK):
             window = windows[t % 3]
@@ -341,20 +346,20 @@ def tile_list_modp_ggelu_noneP_kernel(
                 nc.vector.tensor_tensor(window[:].indirect(offsets[:]), y[:, t - 1, :], gate[:], MULT)
             slot = 2 * (SLICES[t] % 2) + SLICES[t] // 2
             nc.sync.dma_start(rows[slot], window[:])
-            for o in range(len(widths)):
+            for o, w in enumerate(widths):
                 src = window[:, out_cols[o]]
-                if o >= n_pair:
-                    nc.scalar.copy(fin[o][:, :, slot], src)
-                elif t < PACK - 1:
-                    nc.scalar.copy(pairs[o][:, slot // 2, :, slot % 2], src)
-                else:
-                    nc.vector.tensor_copy(pairs[o][:, slot // 2, :, slot % 2], src)
+                paired = PAIRED[o] if o < n_pair else 0
+                if paired:
+                    copy = nc.scalar.copy if t < PACK - 1 else nc.vector.tensor_copy
+                    copy(pairs[o][:, slot // 2, :, slot % 2], src[:, 0:paired])
+                if paired < w:
+                    nc.scalar.copy(fin[o][:, paired:w, slot], src[:, paired:w])
             if t == 0:
                 down_slice(PACK - 1)
 
         for o in range(n_pair):
             nc.vector.tensor_copy(
-                fin[o][:].rearrange("p c t -> p (c t)").bitcast(I32).rearrange("p (c u) -> p c u", u=2),
+                fin[o][:, 0 : PAIRED[o], :].rearrange("p c t -> p (c t)").bitcast(I32).rearrange("p (c u) -> p c u", u=2),
                 pairs[o][:].rearrange("p u c e -> p u (c e)").bitcast(I32).rearrange("p u c -> p c u"),
             )
         out_s = held([P, GROUP], U8, "out_s")

@@ -363,18 +363,20 @@ def tile_list_modp_ggelu_noneP_kernel(
                 pairs[o][:].rearrange("p u c e -> p u (c e)").bitcast(I32).rearrange("p u c -> p c u"),
             )
         out_s = held([P, GROUP], U8, "out_s")
+        out_c = [held([P, GROUP], U32, "out_c%d" % group) for group in range(T // GROUP)]
         for o, w in enumerate(widths):
-            out_c = held([P, w], U32, "out_c%d" % o)
             for lo in range(0, w, PIECE):
                 group, col = divmod(out_cols[o].start + lo, GROUP)
                 nc.vector.quantize_mx(
-                    out=out_c[:, lo : lo + PIECE].bitcast(FP8X4),
+                    out=out_c[group][:, col : col + PIECE].bitcast(FP8X4),
                     scales=out_s[4 * group : P, col : col + PIECE],
                     in_=fin[o][:, lo : lo + PIECE, :].rearrange("p c t -> p (c t)"),
                 )
-            nc.sync.dma_start(
-                out_1[0].rearrange("p t b -> p (t b)").bitcast(I32)[:, out_cols[o]], out_c[:].bitcast(I32)
-            )
+                if col + PIECE == GROUP:
+                    nc.sync.dma_start(
+                        out_1[0].rearrange("p t b -> p (t b)").bitcast(I32)[:, group * GROUP : (group + 1) * GROUP],
+                        out_c[group][:].bitcast(I32),
+                    )
         for q in range(4):
             (nc.scalar, nc.sync)[q % 2].dma_start(
                 out_2[0, 4 * q : 4 * q + 4, :].bitcast(I32).rearrange("r (g c) -> g r c", g=T // GROUP),

@@ -28,7 +28,7 @@ SECOND_H = 3 * ROW_PAIR_BYTES
 LAST_ROUNDED = 4 * ROW_PAIR_BYTES
 SLICES = (1, 0, 2, 3)
 LAST_H = SECOND_H + 2048
-GPSIMD_TOKENS = {4: SUB, 5: SUB // 2}
+GPSIMD_TOKENS = {4: SUB, 5: SUB // 4}
 GROUP = 512
 PIECE = 256
 PIECE_WIDTHS = (512, 512, 512, 256, 256)
@@ -112,10 +112,7 @@ def tile_list_modp_ggelu_noneP_kernel(
 
         nc.vector.tensor_copy(both[0][:], tab_w[:].indirect(entries(0, HALF)))
         part_words(held([P, PASSES, 2 * HALF], U8, "tok_w0"))
-        for c in range(2):
-            nc.vector.tensor_copy(
-                both[1][:, c * CHUNK : (c + 1) * CHUNK], tab_w[:].indirect(entries(HALF + c * CHUNK, CHUNK))
-            )
+        nc.vector.tensor_copy(both[1][:], tab_w[:].indirect(entries(HALF, HALF)))
         wd_raw = held([P, PACK, N], F32, "wd_raw", "tab_w")
         for t in range(PACK):
             nc.sync.dma_start(wd_raw[:, t, :], wd.rearrange("(q t e) n -> t q e n", t=PACK, e=2)[t])

from contextlib import ExitStack

import concourse.mybir as mybir

K, R, N, T, J = 1024, 512, 512, 2048, 1024
FLOPS = 2 * J * (2 * K * R + R * N)

F32 = mybir.dt.float32
BF16 = mybir.dt.bfloat16
I32 = mybir.dt.int32
U32 = mybir.dt.uint32
U16 = mybir.dt.uint16
U8 = mybir.dt.uint8
FP8X4 = mybir.dt.float8_e4m3fn_x4
FP4X4 = mybir.dt.float4_e2m1fn_x4
MULT = mybir.AluOpType.mult
GELU = mybir.ActivationFunctionType.Gelu_apprx_tanh

P = 128
PACK = 4
PASSES = K // (P * PACK)
HALF = 512
CHUNK = 256
SUB = 128
GATES_AHEAD = 3
ROW_PAIR_BYTES = 2 * R * 4
SECOND_H = 3 * ROW_PAIR_BYTES
LAST_ROUNDED = 4 * ROW_PAIR_BYTES
SLICES = (1, 0, 2, 3)
LAST_H = SECOND_H + 2048
GPSIMD_TOKENS = {4: SUB, 5: SUB // 4}
GROUP = 512
PIECE = 256
PIECE_WIDTHS = (512, 512, 512, 256, 256)
PAIRED = (512, 384)


def tile_list_modp_ggelu_noneP_kernel(
    tc, tab_words, tab_scales, wg_words, wg_scales, wu, wd, wgo, offs, out_0, out_1, out_2
):
    nc = tc.nc
    with ExitStack() as ctx:
        keep = ctx.enter_context(tc.tile_pool(name="keep", bufs=1))
        ring = ctx.enter_context(tc.tile_pool(name="ring", bufs=2))
        turns = ctx.enter_context(tc.tile_pool(name="turns", bufs=1))
        psum = ctx.enter_context(tc.psum_pool(name="psum", bufs=1))

        def held(shape, dtype, name, tag=None):
            return keep.tile(shape, dtype, name=name, tag=tag or name, align_bytes=64)

        def placed(shape, dtype, name, offset):
            return turns.tile(shape, dtype, name=name, offset=offset, align_bytes=64)

        def entries(first, count):
            return offsets[:, first // 16 : (first + count) // 16]

        offsets = keep.tile([P, J // 16], U16, name="offsets")
        nc.sync.dma_start(offsets[:], offs)
        tab_s = placed([P, T], U8, "tab_s", ROW_PAIR_BYTES - T // 2)
        nc.sync.dma_start(tab_s[96:128, :].bitcast(I32), tab_scales.rearrange("a q t -> q a t").bitcast(I32))
        tab_w = held([P, T], U32, "tab_w")
        nc.sync.dma_start(tab_w[:].bitcast(I32), tab_words[0].rearrange("p t b -> p (t b)").bitcast(I32))
        wg_raw = held([P, PASSES, 2 * R], U8, "wg_raw")
        nc.sync.dma_start(wg_raw[:].bitcast(I32), wg_words.rearrange("a p c -> p a c").bitcast(I32))

        wu_rows = wu.rearrange("(a p j) c -> a p j c", a=PASSES, j=PACK)
        wu_first = held([P, PACK, R], F32, "wu_first")
        nc.sync.dma_start(wu_first[:], wu_rows[0])

        nc.vector.memset(tab_s[0:96, 0 : T - 4].bitcast(I32), 0)
        nc.vector.memset(tab_s[0:96, T - 4 : T].bitcast(I32), 0)
        wgs_raw = held([P, PASSES, R], U8, "wgs_raw")
        nc.gpsimd.memset(wgs_raw[:].rearrange("p a c -> p (a c)").bitcast(I32), 0)
        for q in range(4):
            nc.scalar.dma_start(
                wgs_raw[32 * q : 32 * q + 4, :, :].bitcast(I32),
                wg_scales[:, 4 * q : 4 * q + 4, :].rearrange("a r c -> r a c").bitcast(I32),
            )
        warm = held([P, 1], F32, "warm")
        warm2 = held([P, 1], F32, "warm2")
        nc.vector.memset(warm[:], 0.0)
        nc.scalar.activation(warm2[:], warm[:], GELU)
        tok_s = held([P, PASSES, J], U8, "tok_s")
        windows = [held([P, T], F32, "window%d" % i) for i in range(2)]
        for window in windows:
            nc.gpsimd.memset(window[:], 0.0)

        picked_s = held([P, J], U8, "picked_s")
        nc.vector.tensor_copy(picked_s[:], tab_s[:].indirect(offsets[:]))

        for q in range(4):
            row = 96 + 8 * q
            nc.sync.dma_start(
                tok_s[32 * q : 32 * q + 4, :, :].rearrange("p a j -> p (a j)").bitcast(I32),
                picked_s[row : row + 8, :].bitcast(I32),
            )
        wu_second = []
        for i in range(2):
            raw = placed([P, 2, R], F32, "wu_second%d" % i, i * ROW_PAIR_BYTES)
            nc.sync.dma_start(raw[:], wu_rows[1][:, 2 * i : 2 * i + 2, :])
            wu_second.append(raw)

        both = [held([P, HALF], U32, "picked_w%d" % h) for h in range(2)]
        tok_w = []

        def part_words(parted):
            picked = both[len(tok_w)]
            nc.vector.tensor_copy(
                parted[:].bitcast(U16), picked[:].bitcast(U16).rearrange("p (j a) -> p a j", a=PASSES)
            )
            tok_w.append(parted)

        nc.vector.tensor_copy(both[0][:], tab_w[:].indirect(entries(0, HALF)))
        part_words(held([P, PASSES, 2 * HALF], U8, "tok_w0"))
        nc.vector.tensor_copy(both[1][:], tab_w[:].indirect(entries(HALF, HALF)))
        wd_raw = held([P, PACK, N], F32, "wd_raw", "tab_w")
        for t in range(PACK):
            nc.sync.dma_start(wd_raw[:, t, :], wd.rearrange("(q t e) n -> t q e n", t=PACK, e=2)[t])
        gate = held([P, J], F32, "gate", "picked_w0")
        nc.sync.dma_start(gate[:], wgo)

        wg_w = held([P, PASSES, 2 * R], U8, "wg_w")
        nc.scalar.copy(
            wg_w[:].bitcast(U32).rearrange("p a (t g i) -> p a g t i", t=PACK, i=4),
            wg_raw[:].bitcast(U32).rearrange("p a (g i t) -> p a g t i", t=PACK, i=4),
        )
        wg_s = held([P, PASSES, R], U8, "wg_s")
        nc.scalar.copy(
            wg_s[:].bitcast(U16).rearrange("p a (t g i) -> p a g t i", t=PACK, i=8),
            wgs_raw[:].bitcast(U16).rearrange("p a (g i t) -> p a g t i", t=PACK, i=8),
        )

        spin = psum.tile([P, HALF], F32, name="spin", tag="turn")
        for i in range(3):
            nc.tensor.matmul_mx(
                out=spin[:],
                lhsT=wg_w[:, 0, 0 : 2 * P].bitcast(FP4X4),
                lhsT_scale=wg_s[:, 0, 0:P],
                rhs=wg_w[:, 0, :].bitcast(FP4X4),
                rhs_scale=wg_s[:, 0, :],
                start=True,
                stop=True,
            )

        def quantised(grouped, name):
            cod = held([P, 2 * P], U32, name + "_codes")
            sca = held([P, 2 * P], U8, name + "_scales")
            nc.vector.quantize_mx(out=cod[:].bitcast(FP8X4), scales=sca[:], in_=grouped[:])
            return cod, sca

        def round_wu(copy, grouped, raw, u, rows, cols):
            copy(
                grouped[:].rearrange("p (t q e j) -> p q j t e", t=2, e=2, j=PACK)[:, cols, rows],
                raw[:].rearrange("p j (q t e) -> p q j t e", t=PACK, e=2)[:, cols, :, 2 * u : 2 * u + 2, :],
            )

        grouped = [
            [held([P, 2 * P * PACK], BF16, "wu_grouped0%d" % u) for u in range(2)],
            [placed([P, 2 * P * PACK], BF16, "wu_grouped10", LAST_ROUNDED), placed([P, 2 * P * PACK], BF16, "wu_grouped11", LAST_ROUNDED + 2048)],
        ]
        round_wu(nc.scalar.copy, grouped[0][0], wu_first, 0, slice(0, 4), slice(0, 64))
        round_wu(nc.vector.tensor_copy, grouped[0][1], wu_first, 1, slice(0, 4), slice(0, 64))
        wu_q = [[quantised(grouped[0][u], "wu0%d" % u) for u in range(2)]]
        for i in range(2):
            shared = (64, 32)[i]
            rows = slice(2 * i, 2 * i + 2)
            round_wu(nc.scalar.copy, grouped[1][0], wu_second[i], 0, rows, slice(0, shared))
            round_wu(nc.vector.tensor_copy, grouped[1][1], wu_second[i], 1, rows, slice(0, 64))
            if shared < 64:
                round_wu(nc.vector.tensor_copy, grouped[1][0], wu_second[i], 0, rows, slice(shared, 64))
        wu_q.append([quantised(grouped[1][u], "wu1%d" % u) for u in (1, 0)][::-1])
        part_words(placed([P, PASSES, 2 * HALF], U8, "tok_w1", LAST_ROUNDED + 2048))

        def round_wd(u, grouped):
            nc.scalar.copy(
                grouped[:].rearrange("p (t q j) -> p q j t", t=2, j=PACK),
                wd_raw[:].rearrange("p j (q e u) -> p q j e u", e=2, u=2)[:, :, :, :, u],
            )
            return grouped

        def stationary(halves, t):
            cod, sca = halves[t // 2]
            cols = slice(P * (t % 2), P * (t % 2 + 1))
            return cod[:, cols].bitcast(FP8X4), sca[:, cols]

        h_b = {0: held([P, CHUNK * PACK], BF16, "h_b0")}
        h_b[1] = placed([P, CHUNK * PACK], BF16, "h_b1", SECOND_H)
        h_c = held([P, J], U32, "h_c")
        h_s = held([P, J], U8, "h_s")
        y = held([P, PACK - 1, J], F32, "y")
        first_acts = placed([P, GATES_AHEAD, SUB * PACK], F32, "first_acts", ROW_PAIR_BYTES)

        last_act = held([P, SUB * PACK], F32, "last_act")
        y_first = {}

        def project(s):
            first = s * SUB
            words = tok_w[first // HALF][:, :, 2 * (first % HALF) : 2 * (first % HALF + SUB)]
            ga = psum.tile([P, PACK, SUB], F32, name="ga", bufs=GATES_AHEAD)
            ub = psum.tile([P, PACK, SUB], F32, name="ub", bufs=3)
            for a in range(PASSES):
                for t in range(PACK):
                    nc.tensor.matmul_mx(
                        out=ga[:, t, :],
                        lhsT=wg_w[:, a, 2 * P * t : 2 * P * (t + 1)].bitcast(FP4X4),
                        lhsT_scale=wg_s[:, a, P * t : P * (t + 1)],
                        rhs=words[:, a, :].bitcast(FP4X4),
                        rhs_scale=tok_s[:, a, first : first + SUB],
                        start=(a, t) == (0, 0),
                        stop=(a, t) == (PASSES - 1, PACK - 1),
                    )
            if s < GATES_AHEAD:
                act = first_acts[:, s, :]
            elif s == J // SUB - 1:
                act = last_act[:]
            else:
                later_act = ring.tile([P, SUB * PACK], F32, name="later_act")
                act = later_act[:]
            flat_act = act
            act = act.rearrange("p (g i t) -> p g t i", t=PACK, i=2)
            nc.scalar.activation(act, ga[:].rearrange("p t (g i) -> p g t i", i=2), GELU)
            for a in range(PASSES):
                for t in (2, 3, 0, 1):
                    w_codes, w_scales = stationary(wu_q[a], t)
                    nc.tensor.matmul_mx(
                        out=ub[:, t, :],
                        lhsT=w_codes,
                        lhsT_scale=w_scales,
                        rhs=words[:, a, :].bitcast(FP4X4),
                        rhs_scale=tok_s[:, a, first : first + SUB],
                        start=(a, t) == (0, 2),
                        stop=(a, t) == (PASSES - 1, 1),
                    )
            sums = ub[:].rearrange("p t (g i) -> p g t i", i=2)
            share = GPSIMD_TOKENS.get(s, 0)
            up = None
            if share:
                up = held([P, share * PACK], F32, "up%d" % s)
                nc.scalar.copy(up[:].rearrange("p (g i t) -> p g t i", t=PACK, i=2), sums[:, 0 : share // 2])
            return sums, act, up, flat_act

        def multiply(s, factors):
            sums, act, up, flat_act = factors
            lo = (s * SUB % CHUNK) * PACK
            dst = h_b[s * SUB // CHUNK][:, lo : lo + SUB * PACK]
            share = GPSIMD_TOKENS.get(s, 0)
            if share:
                nc.gpsimd.tensor_tensor(dst[:, 0 : share * PACK], up[:], flat_act[:, 0 : share * PACK], MULT)
            if share < SUB:
                rest = slice(share // 2, SUB // 2)
                nc.vector.tensor_tensor(
                    dst.rearrange("p (g i t) -> p g t i", t=PACK, i=2)[:, rest], sums[:, rest], act[:, rest], MULT
                )

        def hidden(s):
            multiply(s, project(s))

        def quantise_h(c):
            cols = slice(c * CHUNK, (c + 1) * CHUNK)
            nc.vector.quantize_mx(out=h_c[:, cols].bitcast(FP8X4), scales=h_s[:, cols], in_=h_b[c][:])

        def down(t, first, count, tag=None):
            cols = slice(first, first + count)
            if tag:
                yb = psum.tile([P, HALF], F32, name="yb", tag=tag)
            elif t == 0:
                yb = psum.tile([P, HALF], F32, name="yb", bufs=1)
            else:
                yb = psum.tile([P, HALF], F32, name="late_yb", tag="ub", bufs=3)
            w_codes, w_scales = stationary(wd_q, SLICES[t])
            nc.tensor.matmul_mx(
                out=yb[:, 0:count],
                lhsT=w_codes,
                lhsT_scale=w_scales,
                rhs=h_c[:, cols].bitcast(FP8X4),
                rhs_scale=h_s[:, cols],
                start=True,
                stop=True,
            )
            return yb[:, 0:count]

        def place(c):
            cols = slice(c * CHUNK, (c + 1) * CHUNK)
            nc.vector.tensor_tensor(
                windows[0][:].indirect(entries(c * CHUNK, CHUNK)), y_first[c][:], gate[:, cols], MULT
            )

        def first_slice(c, tag=None):
            y_first[c] = held([P, CHUNK], F32, "y_first%d" % c, tag)
            nc.scalar.copy(y_first[c][:], down(0, c * CHUNK, CHUNK))

        hidden(0)
        hidden(1)
        quantise_h(0)
        hidden(2)
        wd_q = [quantised(round_wd(0, placed([P, 2 * P * PACK], BF16, "wd_grouped0", LAST_ROUNDED - 1024)), "wd0")]
        first_sums = down(0, 0, CHUNK)
        hidden(3)
        fifth = project(4)
        weighted = held([P, CHUNK], F32, "weighted")
        nc.vector.tensor_tensor(weighted[:], first_sums, gate[:, 0:CHUNK], MULT)
        quantise_h(1)
        nc.vector.tensor_copy(windows[0][:].indirect(entries(0, CHUNK)), weighted[:])
        h_b[2] = placed([P, CHUNK * PACK], BF16, "h_b2", SECOND_H - CHUNK * 4)
        multiply(4, fifth)
        hidden(5)
        h_b[3] = placed([P, CHUNK * PACK], BF16, "h_b3", LAST_H)
        hidden(6)
        quantise_h(2)
        first_slice(1, "up5")
        place(1)
        wd_q.append(quantised(round_wd(1, placed([P, 2 * P * PACK], BF16, "wd_grouped1", SECOND_H)), "wd1"))
        hidden(7)
        y_first[2] = held([P, CHUNK], F32, "y_first2")
        nc.scalar.copy(y_first[2][:], down(0, 2 * CHUNK, CHUNK, "turn"))
        place(2)
        quantise_h(3)
        windows.append(placed([P, T], F32, "window2", SECOND_H))
        nc.gpsimd.memset(windows[2][:], 0.0)
        nc.scalar.copy(y[:, 0, 0:HALF], down(1, 0, HALF, "turn"))
        nc.vector.tensor_tensor(windows[1][:].indirect(entries(0, HALF)), y[:, 0, 0:HALF], gate[:, 0:HALF], MULT)
        first_slice(3)
        place(3)
        nc.scalar.copy(y[:, 0, HALF:J], down(1, HALF, HALF))

        def down_slice(t):
            for h in range(2):
                nc.scalar.copy(y[:, t - 1, h * HALF : (h + 1) * HALF], down(t, h * HALF, HALF))

        down_slice(2)

        rows = out_0.rearrange("(p t) c -> t p c", t=PACK)
        widths = PIECE_WIDTHS
        n_pair = len(PAIRED)
        out_cols = [slice(sum(widths[:o]), sum(widths[: o + 1])) for o in range(len(widths))]
        pairs = [held([P, 2, w, 2], BF16, "pairs%d" % o) for o, w in enumerate(PAIRED)]
        fin = [held([P, w, PACK], BF16, "fin%d" % o) for o, w in enumerate(widths)]
        for t in range(PACK):
            window = windows[t % 3]
            if t == 1:
                nc.vector.tensor_tensor(window[:].indirect(entries(HALF, HALF)), y[:, 0, HALF:J], gate[:, HALF:J], MULT)
            elif t > 1:
                nc.vector.tensor_tensor(window[:].indirect(offsets[:]), y[:, t - 1, :], gate[:], MULT)
            slot = 2 * (SLICES[t] % 2) + SLICES[t] // 2
            nc.sync.dma_start(rows[slot], window[:])
            for o, w in enumerate(widths):
                src = window[:, out_cols[o]]
                paired = PAIRED[o] if o < n_pair else 0
                if paired:
                    copy = nc.scalar.copy if t < PACK - 1 else nc.vector.tensor_copy
                    copy(pairs[o][:, slot // 2, :, slot % 2], src[:, 0:paired])
                if paired < w:
                    nc.scalar.copy(fin[o][:, paired:w, slot], src[:, paired:w])
            if t == 0:
                down_slice(PACK - 1)

        for o in range(n_pair):
            nc.vector.tensor_copy(
                fin[o][:, 0 : PAIRED[o], :].rearrange("p c t -> p (c t)").bitcast(I32).rearrange("p (c u) -> p c u", u=2),
                pairs[o][:].rearrange("p u c e -> p u (c e)").bitcast(I32).rearrange("p u c -> p c u"),
            )
        out_s = held([P, GROUP], U8, "out_s")
        out_c = [held([P, GROUP], U32, "out_c%d" % group) for group in range(T // GROUP)]
        for o, w in enumerate(widths):
            for lo in range(0, w, PIECE):
                group, col = divmod(out_cols[o].start + lo, GROUP)
                nc.vector.quantize_mx(
                    out=out_c[group][:, col : col + PIECE].bitcast(FP8X4),
                    scales=out_s[4 * group : P, col : col + PIECE],
                    in_=fin[o][:, lo : lo + PIECE, :].rearrange("p c t -> p (c t)"),
                )
                if col + PIECE == GROUP:
                    nc.sync.dma_start(
                        out_1[0].rearrange("p t b -> p (t b)").bitcast(I32)[:, group * GROUP : (group + 1) * GROUP],
                        out_c[group][:].bitcast(I32),
                    )
        for q in range(4):
            (nc.scalar, nc.sync)[q % 2].dma_start(
                out_2[0, 4 * q : 4 * q + 4, :].bitcast(I32).rearrange("r (g c) -> g r c", g=T // GROUP),
                out_s[32 * q : 32 * q + 16, :].bitcast(I32),
            )
